import numpy as np
import ml_dtypes


def mxq(x, axis, fmt="e4m3"):
    dtype, down = {"e4m3": (ml_dtypes.float8_e4m3fn, 7), "e5m2": (ml_dtypes.float8_e5m2, 14)}[fmt]
    v = np.moveaxis(np.asarray(x, np.float32).astype(ml_dtypes.bfloat16).astype(np.float64), axis, -1)
    blocks = v.reshape(v.shape[:-1] + (-1, 32))
    amax = np.abs(blocks).max(-1, keepdims=True)
    byte = np.maximum(np.where(amax > 0, np.frexp(amax)[1] - 1 + 127, 0) - down, 1)
    scale = np.exp2(byte - 127.0)
    codes = (blocks / scale).astype(np.float32).astype(dtype).astype(np.float64)
    return np.moveaxis((codes * scale).reshape(v.shape), -1, axis)


WIDE = False


def mx_kscale(k):
    if not WIDE:
        return np.ones(k)
    levels = np.array([10, -10, 5, -5, 0])
    if k % 512:
        return np.exp2(np.random.permutation(np.resize(levels, k // 32))).repeat(32)
    a = np.empty((k // 512, 16))
    for p in range(k // 512):
        a[p, :8] = np.random.permutation(np.resize(levels, 8))
        for g in range(8):
            far = levels[np.abs(levels - a[p, g]) >= 10]
            a[p, g + 8] = far[np.random.randint(len(far))]
    return np.exp2(a.ravel()).repeat(32)


def f64(x):
    return np.asarray(x).astype(np.float64)


def striped(idx):
    return np.tile(idx.reshape(-1, 16).T, (8, 1)).astype(np.uint16)


def unstriped(offs):
    return offs[:16].T.reshape(-1).astype(np.int64)


E2M1 = np.array([0.0, 0.5, 1.0, 1.5, 2.0, 3.0, 4.0, 6.0, -0.0, -0.5, -1.0, -1.5, -2.0, -3.0, -4.0, -6.0])


def pack_weight(w, fmt):
    k, n = w.shape
    w = f64(np.asarray(w, np.float32).astype(ml_dtypes.bfloat16)).reshape(k // 32, 32, n)
    amax = np.abs(w).max(1)
    if fmt == "e4m3":
        byte = np.frexp(amax)[1] - 1 + 127 - 7
    else:
        mant, ex = np.frexp(amax / 6.0)
        byte = np.where(mant > 0.5, ex, ex - 1) + 127
    byte = np.clip(np.where(amax > 0, byte, 1), 1, 254)
    scaled = (w * np.exp2(127.0 - byte)[:, None, :]).reshape(k, n).astype(np.float32)
    by_word = np.ascontiguousarray(scaled.reshape(k // 512, 128, 4, n).transpose(0, 1, 3, 2))
    if fmt == "e4m3":
        words = by_word.astype(ml_dtypes.float8_e4m3fn).view(np.uint8)
    else:
        c = by_word.astype(ml_dtypes.float4_e2m1fn).view(np.uint8) & 0xF
        words = (c[..., 0::2] | (c[..., 1::2] << 4)).reshape(k // 512, 128, 2 * n)
    return np.ascontiguousarray(words), np.ascontiguousarray(byte.astype(np.uint8).reshape(k // 512, 16, n))


def unpack_weight(words, scales, fmt):
    g, _, n = scales.shape
    words = np.ascontiguousarray(words).reshape(g, 128, n, -1)
    if fmt == "e4m3":
        vals = words.view(ml_dtypes.float8_e4m3fn).astype(np.float64)
    else:
        nib = np.empty((g, 128, n, 4), np.uint8)
        nib[..., 0::2] = words & 0xF
        nib[..., 1::2] = words >> 4
        vals = E2M1[nib]
    vals = vals * np.repeat(np.exp2(scales.astype(np.float64) - 127.0), 8, axis=1)[..., None]
    return vals.transpose(0, 1, 3, 2).reshape(g * 512, n)


def relu(v):
    return np.maximum(v, 0.0)


K, T, S, H, N = 512, 2048, 1024, 512, 256


def setup_inputs():
    n = np.random.standard_normal
    s = mx_kscale(K)
    u = mx_kscale(H)
    hard = np.random.permutation(T)[:S]
    x = pack_weight(n((K, T)) * s[:, None], "e4m3")
    w = pack_weight(n((K, N)) / np.sqrt(K) / s[:, None], "e2m1")
    return {
        "x_words": x[0],
        "x_scales": x[1],
        "w_words": w[0],
        "w_scales": w[1],
        "w1": (n((K, H)) / np.sqrt(K) / s[:, None]).astype(np.float32),
        "w3": (n((K, H)) / np.sqrt(K) / s[:, None] * u).astype(np.float32),
        "w2": (n((H, N)) / np.sqrt(H) / u[:, None]).astype(np.float32),
        "offs": striped(hard),
    }


def reference(x_words, x_scales, w_words, w_scales, w1, w3, w2, offs):
    w = unpack_weight(w_words, w_scales, "e2m1")
    w1q = mxq(f64(w1), 0, "e4m3")
    w3q = mxq(f64(w3), 0, "e4m3")
    w2q = mxq(f64(w2), 0, "e4m3")
    idx = unstriped(offs)
    x = unpack_weight(x_words, x_scales, "e4m3")
    out = w.T @ x
    h = relu(w1q.T @ x[:, idx]) * (w3q.T @ x[:, idx])
    out[:, idx] = w2q.T @ mxq(h, 0, "e4m3")
    return out

@@ -1,0 +1,181 @@
+from contextlib import ExitStack
+
+import concourse.mybir as mybir
+
+K, T, S, H, N = 512, 2048, 1024, 512, 256
+FLOPS = 2 * K * N * T + 2 * 2 * K * H * S + 2 * H * N * S
+
+F32 = mybir.dt.float32
+BF16 = mybir.dt.bfloat16
+I32 = mybir.dt.int32
+U32 = mybir.dt.uint32
+U16 = mybir.dt.uint16
+U8 = mybir.dt.uint8
+FP8X4 = mybir.dt.float8_e4m3fn_x4
+FP4X4 = mybir.dt.float4_e2m1fn_x4
+RELU = mybir.ActivationFunctionType.Relu
+MULT = mybir.AluOpType.mult
+
+P = 128
+PACK = 4
+BANK = 512
+GROUP = 128
+CHUNK = 256
+HALF = H // 2
+
+
+def load_scale_rows(nc, plane, scales):
+    rows = scales[0].rearrange("(q r) c -> r q c", r=4)
+    for r in range(4):
+        nc.sync.dma_start(out=plane[r:P:32, :].bitcast(I32), in_=rows[r].bitcast(I32))
+
+
+def tile_moe_cas_glu_relu_kernel(tc, x_words, x_scales, w_words, w_scales, w1, w3, w2, offs, out):
+    nc = tc.nc
+    with ExitStack() as ctx:
+        keep = ctx.enter_context(tc.tile_pool(name="keep", bufs=1))
+        ring = ctx.enter_context(tc.tile_pool(name="ring", bufs=4))
+        psum = ctx.enter_context(tc.psum_pool(name="psum", bufs=2))
+        deep = ctx.enter_context(tc.psum_pool(name="deep", bufs=4))
+
+        offsets = keep.tile([P, S // 16], U16, name="offsets")
+        x_plane = keep.tile([P, T], U8, name="x_plane", align_bytes=64)
+        w_plane = keep.tile([P, N], U8, name="w_plane", align_bytes=64)
+        x_codes = keep.tile([P, T], I32, name="x_codes", align_bytes=64)
+        w_codes = keep.tile([P, 2 * N], U8, name="w_codes", align_bytes=64)
+        nc.vector.memset(x_plane[:].bitcast(I32), 0)
+        nc.vector.memset(w_plane[:].bitcast(I32), 0)
+
+        raw = {(name, half): keep.tile([P, PACK, HALF], F32, name=f"{name}_raw{half}") for name in ("w1", "w3") for half in range(2)}
+        w2_raw = keep.tile([P, PACK, N], F32, name="w2_raw")
+
+        def load_half(name, w, half):
+            nc.sync.dma_start(out=raw[name, half][:], in_=w[:, half * HALF : (half + 1) * HALF].rearrange("(p j) c -> p j c", j=PACK))
+
+        load_half("w1", w1, 0)
+        load_scale_rows(nc, x_plane, x_scales)
+        nc.sync.dma_start(offsets[:], offs)
+        nc.sync.dma_start(out=w_codes[:].bitcast(I32), in_=w_words[0].bitcast(I32))
+        nc.sync.dma_start(out=x_codes[:], in_=x_words[0].rearrange("p t d -> p (t d)").bitcast(I32))
+        load_scale_rows(nc, w_plane, w_scales)
+        load_half("w1", w1, 1)
+        load_half("w3", w3, 0)
+        load_half("w3", w3, 1)
+        nc.sync.dma_start(out=w2_raw[:], in_=w2.rearrange("(p j) c -> p j c", j=PACK))
+
+        slot_plane = keep.tile([P, S], U8, name="slot_plane", align_bytes=64)
+        slot_codes = keep.tile([P, S], U32, name="slot_codes", align_bytes=64)
+        nc.vector.tensor_copy(slot_plane[:], x_plane[:].indirect(offsets[:]))
+        nc.vector.tensor_copy(slot_codes[:], x_codes[:].bitcast(U32).indirect(offsets[:]))
+
+        windows = [keep.tile([P, T], F32, name=f"window{b}") for b in range(N // P)]
+
+        def light(b, c):
+            cols = slice(c * BANK, (c + 1) * BANK)
+            y = psum.tile([P, BANK], F32, name="y", tag="result")
+            nc.tensor.matmul_mx(
+                out=y[:],
+                lhsT=w_codes[:, 2 * P * b : 2 * P * (b + 1)].bitcast(FP4X4),
+                lhsT_scale=w_plane[:, P * b : P * (b + 1)],
+                rhs=x_codes[:, cols].bitcast(FP8X4),
+                rhs_scale=x_plane[:, cols],
+                start=True,
+                stop=True,
+            )
+            nc.scalar.copy(out=windows[b][:, cols], in_=y[:])
+
+        grouped = {name: keep.tile([P, PACK, P, PACK], BF16, name=f"{name}_grouped", align_bytes=64) for name in ("w1", "w3")}
+        codes = {name: keep.tile([P, H], U32, name=f"{name}_codes", align_bytes=64) for name in ("w1", "w3")}
+        plane = {name: keep.tile([P, H], U8, name=f"{name}_plane", align_bytes=64) for name in ("w1", "w3")}
+
+        def regroup(copy, name, half):
+            m = slice(half * P // 2, (half + 1) * P // 2)
+            copy(out=grouped[name][:, :, m, :].rearrange("p t m j -> p m j t"), in_=raw[name, half][:].rearrange("p j (m t) -> p m j t", t=PACK))
+
+        def quantize_first(name):
+            nc.vector.quantize_mx(out=codes[name][:].bitcast(FP8X4), scales=plane[name][:], in_=grouped[name][:].rearrange("p t m j -> p (t m j)"))
+
+        regroup(nc.scalar.copy, "w1", 0)
+        regroup(nc.vector.tensor_copy, "w1", 1)
+        regroup(nc.scalar.copy, "w3", 0)
+        for c in range(4):
+            light(0, c)
+        quantize_first("w1")
+        regroup(nc.vector.tensor_copy, "w3", 1)
+        quantize_first("w3")
+
+        w2_grouped = keep.tile([P, N, PACK], BF16, name="w2_grouped", align_bytes=64)
+        w2_codes = keep.tile([P, N], U32, name="w2_codes", align_bytes=64)
+        w2_plane = keep.tile([P, N], U8, name="w2_plane", align_bytes=64)
+        z = keep.tile([P, N // P, S], F32, name="z")
+        nc.vector.tensor_copy(out=w2_grouped[:].rearrange("p (c i) j -> p c j i", i=4), in_=w2_raw[:].rearrange("p j (c i) -> p c j i", i=4))
+
+        def first_product(pool, name, g):
+            cols = slice(g * GROUP, (g + 1) * GROUP)
+            acc = pool.tile([P, PACK, GROUP], F32, name=f"{name}_acc")
+            for t in range(PACK):
+                nc.tensor.matmul_mx(
+                    out=acc[:, t, :],
+                    lhsT=codes[name][:, t * P : (t + 1) * P].bitcast(FP8X4),
+                    lhsT_scale=plane[name][:, t * P : (t + 1) * P],
+                    rhs=slot_codes[:, cols].bitcast(FP8X4),
+                    rhs_scale=slot_plane[:, cols],
+                    start=True,
+                    stop=True,
+                )
+            return acc
+
+        def hidden(h, g):
+            a1 = first_product(psum, "w1", g)
+            gate = ring.tile([P, GROUP, PACK], F32, name="gate")
+            nc.scalar.activation(out=gate[:], in_=a1[:].rearrange("p t s -> p s t"), func=RELU)
+            a3 = first_product(deep, "w3", g)
+            part = g % (CHUNK // GROUP)
+            nc.vector.tensor_tensor(out=h[:, part * GROUP : (part + 1) * GROUP, :], in0=a3[:].rearrange("p t s -> p s t"), in1=gate[:], op=MULT)
+
+        h_codes = keep.tile([P, S], U32, name="h_codes", align_bytes=64)
+        h_plane = keep.tile([P, S], U8, name="h_plane", align_bytes=64)
+
+        def quantize_hidden(h, c):
+            cols = slice(c * CHUNK, (c + 1) * CHUNK)
+            nc.vector.quantize_mx(out=h_codes[:, cols].bitcast(FP8X4), scales=h_plane[:, cols], in_=h[:].rearrange("p s t -> p (s t)"))
+
+        def second(b, c):
+            cols = slice(c * BANK, (c + 1) * BANK)
+            acc = psum.tile([P, BANK], F32, name="z_acc", tag="result")
+            nc.tensor.matmul_mx(
+                out=acc[:],
+                lhsT=w2_codes[:, b * P : (b + 1) * P].bitcast(FP8X4),
+                lhsT_scale=w2_plane[:, b * P : (b + 1) * P],
+                rhs=h_codes[:, cols].bitcast(FP8X4),
+                rhs_scale=h_plane[:, cols],
+                start=True,
+                stop=True,
+            )
+            nc.scalar.copy(out=z[:, b, cols], in_=acc[:])
+
+        def scatter(b, lo, hi):
+            nc.vector.tensor_copy(windows[b][:].indirect(offsets[:, lo // 16 : hi // 16]), z[:, b, lo:hi])
+
+        hs = [ring.tile([P, CHUNK, PACK], BF16, name="h", align_bytes=64) for c in range(S // CHUNK)]
+        hidden(hs[0], 0)
+        hidden(hs[0], 1)
+        nc.vector.quantize_mx(out=w2_codes[:].bitcast(FP8X4), scales=w2_plane[:], in_=w2_grouped[:].rearrange("p n j -> p (n j)"))
+        for c in range(1, S // CHUNK):
+            hidden(hs[c], 2 * c)
+            quantize_hidden(hs[c - 1], c - 1)
+            hidden(hs[c], 2 * c + 1)
+        quantize_hidden(hs[-1], S // CHUNK - 1)
+        second(0, 0)
+        for c in range(4):
+            light(1, c)
+        second(1, 0)
+        second(0, 1)
+        second(1, 1)
+
+        scatter(0, 0, S // 2)
+        scatter(1, 0, S // 4)
+        scatter(0, S // 2, S)
+        nc.sync.dma_start(out=out[0:P, :], in_=windows[0][:])
+        scatter(1, S // 4, S)
+        nc.sync.dma_start(out=out[P : 2 * P, :], in_=windows[1][:])

@@ -35,6 +35,7 @@ def tile_moe_cas_glu_relu_kernel(tc, x_words, x_scales, w_words, w_scales, w1, w
     with ExitStack() as ctx:
         keep = ctx.enter_context(tc.tile_pool(name="keep", bufs=1))
         ring = ctx.enter_context(tc.tile_pool(name="ring", bufs=4))
+        stage = ctx.enter_context(tc.tile_pool(name="stage", bufs=3))
         psum = ctx.enter_context(tc.psum_pool(name="psum", bufs=2))
         deep = ctx.enter_context(tc.psum_pool(name="deep", bufs=4))
 
@@ -46,8 +47,10 @@ def tile_moe_cas_glu_relu_kernel(tc, x_words, x_scales, w_words, w_scales, w1, w
         nc.vector.memset(x_plane[:].bitcast(I32), 0)
         nc.vector.memset(w_plane[:].bitcast(I32), 0)
 
-        raw = {(name, half): keep.tile([P, PACK, HALF], F32, name=f"{name}_raw{half}") for name in ("w1", "w3") for half in range(2)}
-        w2_raw = keep.tile([P, PACK, N], F32, name="w2_raw")
+        raw = {("w1", half): keep.tile([P, PACK, HALF], F32, name=f"w1_raw{half}") for half in range(2)}
+        for half in range(2):
+            raw["w3", half] = stage.tile([P, PACK, HALF], F32, name=f"w3_raw{half}", tag="stage")
+        w2_raw = stage.tile([P, PACK, N], F32, name="w2_raw", tag="stage")
 
         def load_half(name, w, half):
             nc.sync.dma_start(out=raw[name, half][:], in_=w[:, half * HALF : (half + 1) * HALF].rearrange("(p j) c -> p j c", j=PACK))
@@ -55,10 +58,10 @@ def tile_moe_cas_glu_relu_kernel(tc, x_words, x_scales, w_words, w_scales, w1, w
         load_half("w1", w1, 0)
         load_scale_rows(nc, x_plane, x_scales)
         nc.sync.dma_start(offsets[:], offs)
-        nc.sync.dma_start(out=w_codes[:].bitcast(I32), in_=w_words[0].bitcast(I32))
-        nc.sync.dma_start(out=x_codes[:], in_=x_words[0].rearrange("p t d -> p (t d)").bitcast(I32))
-        load_scale_rows(nc, w_plane, w_scales)
         load_half("w1", w1, 1)
+        nc.sync.dma_start(out=x_codes[:], in_=x_words[0].rearrange("p t d -> p (t d)").bitcast(I32))
+        nc.sync.dma_start(out=w_codes[:].bitcast(I32), in_=w_words[0].bitcast(I32))
+        load_scale_rows(nc, w_plane, w_scales)
         load_half("w3", w3, 0)
         load_half("w3", w3, 1)
         nc.sync.dma_start(out=w2_raw[:], in_=w2.rearrange("(p j) c -> p j c", j=PACK))
@@ -66,13 +69,12 @@ def tile_moe_cas_glu_relu_kernel(tc, x_words, x_scales, w_words, w_scales, w1, w
         slot_plane = keep.tile([P, S], U8, name="slot_plane", align_bytes=64)
         slot_codes = keep.tile([P, S], U32, name="slot_codes", align_bytes=64)
         nc.vector.tensor_copy(slot_plane[:], x_plane[:].indirect(offsets[:]))
-        nc.vector.tensor_copy(slot_codes[:], x_codes[:].bitcast(U32).indirect(offsets[:]))
 
         windows = [keep.tile([P, T], F32, name=f"window{b}") for b in range(N // P)]
 
-        def light(b, c):
+        def light(b, c, tag):
             cols = slice(c * BANK, (c + 1) * BANK)
-            y = psum.tile([P, BANK], F32, name="y", tag="result")
+            y = psum.tile([P, BANK], F32, name="y", tag=tag)
             nc.tensor.matmul_mx(
                 out=y[:],
                 lhsT=w_codes[:, 2 * P * b : 2 * P * (b + 1)].bitcast(FP4X4),
@@ -90,19 +92,23 @@ def tile_moe_cas_glu_relu_kernel(tc, x_words, x_scales, w_words, w_scales, w1, w
 
         def regroup(copy, name, half):
             m = slice(half * P // 2, (half + 1) * P // 2)
-            copy(out=grouped[name][:, :, m, :].rearrange("p t m j -> p m j t"), in_=raw[name, half][:].rearrange("p j (m t) -> p m j t", t=PACK))
+            copy(out=grouped[name][:, :, m, :].rearrange("p t m j -> p m t j"), in_=raw[name, half][:].rearrange("p j (m t) -> p m t j", t=PACK))
 
-        def quantize_first(name):
-            nc.vector.quantize_mx(out=codes[name][:].bitcast(FP8X4), scales=plane[name][:], in_=grouped[name][:].rearrange("p t m j -> p (t m j)"))
+        def quantize_first(name, pieces):
+            step = PACK // pieces
+            for t in range(0, PACK, step):
+                cols = slice(t * P, (t + step) * P)
+                nc.vector.quantize_mx(out=codes[name][:, cols].bitcast(FP8X4), scales=plane[name][:, cols], in_=grouped[name][:, t : t + step].rearrange("p t m j -> p (t m j)"))
 
         regroup(nc.scalar.copy, "w1", 0)
-        regroup(nc.vector.tensor_copy, "w1", 1)
+        regroup(nc.scalar.copy, "w1", 1)
+        quantize_first("w1", 1)
+        nc.vector.tensor_copy(slot_codes[:], x_codes[:].bitcast(U32).indirect(offsets[:]))
         regroup(nc.scalar.copy, "w3", 0)
-        for c in range(4):
-            light(0, c)
-        quantize_first("w1")
+        light(0, 0, "w1")
+        light(0, 1, "w1")
         regroup(nc.vector.tensor_copy, "w3", 1)
-        quantize_first("w3")
+        quantize_first("w3", 4)
 
         w2_grouped = keep.tile([P, N, PACK], BF16, name="w2_grouped", align_bytes=64)
         w2_codes = keep.tile([P, N], U32, name="w2_codes", align_bytes=64)
@@ -112,7 +118,7 @@ def tile_moe_cas_glu_relu_kernel(tc, x_words, x_scales, w_words, w_scales, w1, w
 
         def first_product(pool, name, g):
             cols = slice(g * GROUP, (g + 1) * GROUP)
-            acc = pool.tile([P, PACK, GROUP], F32, name=f"{name}_acc")
+            acc = pool.tile([P, PACK, GROUP], F32, name=f"{name}_acc", tag=name)
             for t in range(PACK):
                 nc.tensor.matmul_mx(
                     out=acc[:, t, :],
@@ -127,7 +133,7 @@ def tile_moe_cas_glu_relu_kernel(tc, x_words, x_scales, w_words, w_scales, w1, w
 
         def hidden(h, g):
             a1 = first_product(psum, "w1", g)
-            gate = ring.tile([P, GROUP, PACK], F32, name="gate")
+            gate = stage.tile([P, GROUP, PACK], F32, name="gate", tag="stage")
             nc.scalar.activation(out=gate[:], in_=a1[:].rearrange("p t s -> p s t"), func=RELU)
             a3 = first_product(deep, "w3", g)
             part = g % (CHUNK // GROUP)
@@ -159,8 +165,10 @@ def tile_moe_cas_glu_relu_kernel(tc, x_words, x_scales, w_words, w_scales, w1, w
 
         hs = [ring.tile([P, CHUNK, PACK], BF16, name="h", align_bytes=64) for c in range(S // CHUNK)]
         hidden(hs[0], 0)
-        hidden(hs[0], 1)
         nc.vector.quantize_mx(out=w2_codes[:].bitcast(FP8X4), scales=w2_plane[:], in_=w2_grouped[:].rearrange("p n j -> p (n j)"))
+        hidden(hs[0], 1)
+        light(0, 2, "result")
+        light(0, 3, "result")
         for c in range(1, S // CHUNK):
             hidden(hs[c], 2 * c)
             quantize_hidden(hs[c - 1], c - 1)
@@ -168,7 +176,7 @@ def tile_moe_cas_glu_relu_kernel(tc, x_words, x_scales, w_words, w_scales, w1, w
         quantize_hidden(hs[-1], S // CHUNK - 1)
         second(0, 0)
         for c in range(4):
-            light(1, c)
+            light(1, c, "result")
         second(1, 0)
         second(0, 1)
         second(1, 1)

@@ -92,7 +92,7 @@ def tile_moe_cas_glu_relu_kernel(tc, x_words, x_scales, w_words, w_scales, w1, w
 
         def regroup(copy, name, half):
             m = slice(half * P // 2, (half + 1) * P // 2)
-            copy(out=grouped[name][:, :, m, :].rearrange("p t m j -> p m t j"), in_=raw[name, half][:].rearrange("p j (m t) -> p m t j", t=PACK))
+            copy(out=grouped[name][:, :, m, :].rearrange("p t m j -> p m j t"), in_=raw[name, half][:].rearrange("p j (m t) -> p m j t", t=PACK))
 
         def quantize_first(name, pieces):
             step = PACK // pieces
@@ -186,4 +186,5 @@ def tile_moe_cas_glu_relu_kernel(tc, x_words, x_scales, w_words, w_scales, w1, w
         scatter(0, S // 2, S)
         nc.sync.dma_start(out=out[0:P, :], in_=windows[0][:])
         scatter(1, S // 4, S)
-        nc.sync.dma_start(out=out[P : 2 * P, :], in_=windows[1][:])
+        nc.sync.dma_start(out=out[P : 2 * P, : T // 2], in_=windows[1][:, : T // 2])
+        nc.scalar.dma_start(out=out[P : 2 * P, T // 2 :], in_=windows[1][:, T // 2 :])

@@ -15,6 +15,7 @@ FP8X4 = mybir.dt.float8_e4m3fn_x4
 FP4X4 = mybir.dt.float4_e2m1fn_x4
 RELU = mybir.ActivationFunctionType.Relu
 MULT = mybir.AluOpType.mult
+ADD = mybir.AluOpType.add
 
 P = 128
 PACK = 4
@@ -34,10 +35,13 @@ def tile_moe_cas_glu_relu_kernel(tc, x_words, x_scales, w_words, w_scales, w1, w
     nc = tc.nc
     with ExitStack() as ctx:
         keep = ctx.enter_context(tc.tile_pool(name="keep", bufs=1))
-        ring = ctx.enter_context(tc.tile_pool(name="ring", bufs=4))
-        stage = ctx.enter_context(tc.tile_pool(name="stage", bufs=3))
-        psum = ctx.enter_context(tc.psum_pool(name="psum", bufs=2))
-        deep = ctx.enter_context(tc.psum_pool(name="deep", bufs=4))
+        psum = ctx.enter_context(tc.psum_pool(name="psum", bufs=1))
+
+        def banks(name):
+            return [psum.tile([P, BANK], F32, name=f"{name}{i}") for i in range(2)]
+
+        sums = {"w1": banks("a1_bank"), "w3": banks("a3_bank")}
+        y_banks, z_banks = banks("y_bank"), banks("z_bank")
 
         offsets = keep.tile([P, S // 16], U16, name="offsets")
         x_plane = keep.tile([P, T], U8, name="x_plane", align_bytes=64)
@@ -47,10 +51,8 @@ def tile_moe_cas_glu_relu_kernel(tc, x_words, x_scales, w_words, w_scales, w1, w
         nc.vector.memset(x_plane[:].bitcast(I32), 0)
         nc.vector.memset(w_plane[:].bitcast(I32), 0)
 
-        raw = {("w1", half): keep.tile([P, PACK, HALF], F32, name=f"w1_raw{half}") for half in range(2)}
-        for half in range(2):
-            raw["w3", half] = stage.tile([P, PACK, HALF], F32, name=f"w3_raw{half}", tag="stage")
-        w2_raw = stage.tile([P, PACK, N], F32, name="w2_raw", tag="stage")
+        raw = {(name, half): keep.tile([P, PACK, HALF], F32, name=f"{name}_raw{half}") for name in ("w1", "w3") for half in range(2)}
+        w2_raw = keep.tile([P, PACK, N], F32, name="w2_raw")
 
         def load_half(name, w, half):
             nc.sync.dma_start(out=raw[name, half][:], in_=w[:, half * HALF : (half + 1) * HALF].rearrange("(p j) c -> p j c", j=PACK))
@@ -58,10 +60,10 @@ def tile_moe_cas_glu_relu_kernel(tc, x_words, x_scales, w_words, w_scales, w1, w
         load_half("w1", w1, 0)
         load_scale_rows(nc, x_plane, x_scales)
         nc.sync.dma_start(offsets[:], offs)
-        load_half("w1", w1, 1)
         nc.sync.dma_start(out=x_codes[:], in_=x_words[0].rearrange("p t d -> p (t d)").bitcast(I32))
         nc.sync.dma_start(out=w_codes[:].bitcast(I32), in_=w_words[0].bitcast(I32))
         load_scale_rows(nc, w_plane, w_scales)
+        load_half("w1", w1, 1)
         load_half("w3", w3, 0)
         load_half("w3", w3, 1)
         nc.sync.dma_start(out=w2_raw[:], in_=w2.rearrange("(p j) c -> p j c", j=PACK))
@@ -69,59 +71,61 @@ def tile_moe_cas_glu_relu_kernel(tc, x_words, x_scales, w_words, w_scales, w1, w
         slot_plane = keep.tile([P, S], U8, name="slot_plane", align_bytes=64)
         slot_codes = keep.tile([P, S], U32, name="slot_codes", align_bytes=64)
         nc.vector.tensor_copy(slot_plane[:], x_plane[:].indirect(offsets[:]))
+        nc.vector.tensor_copy(slot_codes[:], x_codes[:].bitcast(U32).indirect(offsets[:]))
 
         windows = [keep.tile([P, T], F32, name=f"window{b}") for b in range(N // P)]
 
-        def light(b, c, tag):
-            cols = slice(c * BANK, (c + 1) * BANK)
-            y = psum.tile([P, BANK], F32, name="y", tag=tag)
-            nc.tensor.matmul_mx(
-                out=y[:],
-                lhsT=w_codes[:, 2 * P * b : 2 * P * (b + 1)].bitcast(FP4X4),
-                lhsT_scale=w_plane[:, P * b : P * (b + 1)],
-                rhs=x_codes[:, cols].bitcast(FP8X4),
-                rhs_scale=x_plane[:, cols],
-                start=True,
-                stop=True,
-            )
-            nc.scalar.copy(out=windows[b][:, cols], in_=y[:])
+        def light(b):
+            for c in range(T // BANK):
+                cols = slice(c * BANK, (c + 1) * BANK)
+                y = y_banks[c % 2]
+                nc.tensor.matmul_mx(
+                    out=y[:],
+                    lhsT=w_codes[:, 2 * P * b : 2 * P * (b + 1)].bitcast(FP4X4),
+                    lhsT_scale=w_plane[:, P * b : P * (b + 1)],
+                    rhs=x_codes[:, cols].bitcast(FP8X4),
+                    rhs_scale=x_plane[:, cols],
+                    start=True,
+                    stop=True,
+                )
+                nc.scalar.copy(out=windows[b][:, cols], in_=y[:])
 
-        grouped = {name: keep.tile([P, PACK, P, PACK], BF16, name=f"{name}_grouped", align_bytes=64) for name in ("w1", "w3")}
+        grouped = {name: keep.tile([P, PACK * H], BF16, name=f"{name}_grouped", align_bytes=64) for name in ("w1", "w3")}
         codes = {name: keep.tile([P, H], U32, name=f"{name}_codes", align_bytes=64) for name in ("w1", "w3")}
         plane = {name: keep.tile([P, H], U8, name=f"{name}_plane", align_bytes=64) for name in ("w1", "w3")}
 
-        def regroup(copy, name, half):
+        def round_on_gpsimd(out, in_):
+            nc.gpsimd.tensor_scalar(out=out, in0=in_, scalar1=1.0, scalar2=0.0, op0=MULT, op1=ADD)
+
+        def regroup(copy, name, half, walk="m j t"):
             m = slice(half * P // 2, (half + 1) * P // 2)
-            copy(out=grouped[name][:, :, m, :].rearrange("p t m j -> p m j t"), in_=raw[name, half][:].rearrange("p j (m t) -> p m j t", t=PACK))
+            whole = grouped[name][:].rearrange("p (t m j) -> p t m j", t=PACK, j=PACK)
+            copy(out=whole[:, :, m, :].rearrange(f"p t m j -> p {walk}"), in_=raw[name, half][:].rearrange(f"p j (m t) -> p {walk}", t=PACK))
 
         def quantize_first(name, pieces):
-            step = PACK // pieces
-            for t in range(0, PACK, step):
-                cols = slice(t * P, (t + step) * P)
-                nc.vector.quantize_mx(out=codes[name][:, cols].bitcast(FP8X4), scales=plane[name][:, cols], in_=grouped[name][:, t : t + step].rearrange("p t m j -> p (t m j)"))
+            step = H // pieces
+            for lo in range(0, H, step):
+                cols = slice(lo, lo + step)
+                nc.vector.quantize_mx(out=codes[name][:, cols].bitcast(FP8X4), scales=plane[name][:, cols], in_=grouped[name][:, PACK * lo : PACK * (lo + step)])
 
         regroup(nc.scalar.copy, "w1", 0)
-        regroup(nc.scalar.copy, "w1", 1)
+        regroup(round_on_gpsimd, "w1", 1, "t m j")
         quantize_first("w1", 1)
-        nc.vector.tensor_copy(slot_codes[:], x_codes[:].bitcast(U32).indirect(offsets[:]))
-        regroup(nc.scalar.copy, "w3", 0)
-        light(0, 0, "w1")
-        light(0, 1, "w1")
+        regroup(nc.vector.tensor_copy, "w3", 0)
         regroup(nc.vector.tensor_copy, "w3", 1)
         quantize_first("w3", 4)
+        light(0)
 
-        w2_grouped = keep.tile([P, N, PACK], BF16, name="w2_grouped", align_bytes=64)
         w2_codes = keep.tile([P, N], U32, name="w2_codes", align_bytes=64)
         w2_plane = keep.tile([P, N], U8, name="w2_plane", align_bytes=64)
-        z = keep.tile([P, N // P, S], F32, name="z")
-        nc.vector.tensor_copy(out=w2_grouped[:].rearrange("p (c i) j -> p c j i", i=4), in_=w2_raw[:].rearrange("p j (c i) -> p c j i", i=4))
+        round_on_gpsimd(out=grouped["w3"][:, PACK * N :].rearrange("p (n j) -> p n j", j=PACK), in_=w2_raw[:].rearrange("p j n -> p n j"))
 
-        def first_product(pool, name, g):
+        def first_product(name, g):
             cols = slice(g * GROUP, (g + 1) * GROUP)
-            acc = pool.tile([P, PACK, GROUP], F32, name=f"{name}_acc", tag=name)
+            acc = sums[name][g % 2]
             for t in range(PACK):
                 nc.tensor.matmul_mx(
-                    out=acc[:, t, :],
+                    out=acc[:, t * GROUP : (t + 1) * GROUP],
                     lhsT=codes[name][:, t * P : (t + 1) * P].bitcast(FP8X4),
                     lhsT_scale=plane[name][:, t * P : (t + 1) * P],
                     rhs=slot_codes[:, cols].bitcast(FP8X4),
@@ -129,62 +133,81 @@ def tile_moe_cas_glu_relu_kernel(tc, x_words, x_scales, w_words, w_scales, w1, w
                     start=True,
                     stop=True,
                 )
-            return acc
+            return acc[:].rearrange("p (t s) -> p s t", t=PACK)
 
-        def hidden(h, g):
-            a1 = first_product(psum, "w1", g)
-            gate = stage.tile([P, GROUP, PACK], F32, name="gate", tag="stage")
-            nc.scalar.activation(out=gate[:], in_=a1[:].rearrange("p t s -> p s t"), func=RELU)
-            a3 = first_product(deep, "w3", g)
-            part = g % (CHUNK // GROUP)
-            nc.vector.tensor_tensor(out=h[:, part * GROUP : (part + 1) * GROUP, :], in0=a3[:].rearrange("p t s -> p s t"), in1=gate[:], op=MULT)
+        gates = [keep.tile([P, GROUP * PACK], F32, name=f"gate{g}") for g in range(S // GROUP)]
+        ups = {g: keep.tile([P, GROUP * PACK], F32, name=f"up{g}") for g in range(4, S // GROUP)}
+
+        def by_slot(ap):
+            return ap.rearrange("p (s t) -> p s t", t=PACK)
+
+        def part(h, g):
+            lo = g % (CHUNK // GROUP) * GROUP * PACK
+            return h[:, lo : lo + GROUP * PACK]
+
+        def hidden_on_vector(h, g):
+            nc.scalar.activation(out=by_slot(gates[g][:]), in_=first_product("w1", g), func=RELU)
+            nc.vector.tensor_tensor(out=by_slot(part(h, g)), in0=first_product("w3", g), in1=by_slot(gates[g][:]), op=MULT)
+
+        def hidden_on_gpsimd(h, g):
+            nc.scalar.activation(out=by_slot(gates[g][:]), in_=first_product("w1", g), func=RELU)
+            nc.scalar.copy(out=by_slot(ups[g][:]), in_=first_product("w3", g))
+            nc.gpsimd.tensor_tensor(out=part(h, g), in0=ups[g][:], in1=gates[g][:], op=MULT)
 
         h_codes = keep.tile([P, S], U32, name="h_codes", align_bytes=64)
         h_plane = keep.tile([P, S], U8, name="h_plane", align_bytes=64)
 
         def quantize_hidden(h, c):
             cols = slice(c * CHUNK, (c + 1) * CHUNK)
-            nc.vector.quantize_mx(out=h_codes[:, cols].bitcast(FP8X4), scales=h_plane[:, cols], in_=h[:].rearrange("p s t -> p (s t)"))
+            nc.vector.quantize_mx(out=h_codes[:, cols].bitcast(FP8X4), scales=h_plane[:, cols], in_=h[:])
 
-        def second(b, c):
-            cols = slice(c * BANK, (c + 1) * BANK)
-            acc = psum.tile([P, BANK], F32, name="z_acc", tag="result")
+        def second(acc, b, lo, hi):
             nc.tensor.matmul_mx(
-                out=acc[:],
+                out=acc,
                 lhsT=w2_codes[:, b * P : (b + 1) * P].bitcast(FP8X4),
                 lhsT_scale=w2_plane[:, b * P : (b + 1) * P],
-                rhs=h_codes[:, cols].bitcast(FP8X4),
-                rhs_scale=h_plane[:, cols],
+                rhs=h_codes[:, lo:hi].bitcast(FP8X4),
+                rhs_scale=h_plane[:, lo:hi],
                 start=True,
                 stop=True,
             )
-            nc.scalar.copy(out=z[:, b, cols], in_=acc[:])
 
-        def scatter(b, lo, hi):
-            nc.vector.tensor_copy(windows[b][:].indirect(offsets[:, lo // 16 : hi // 16]), z[:, b, lo:hi])
+        def scatter(b, lo, z, acc):
+            nc.scalar.copy(out=z, in_=acc)
+            nc.vector.tensor_copy(windows[b][:].indirect(offsets[:, lo // 16 : (lo + z.shape[1]) // 16]), z)
 
-        hs = [ring.tile([P, CHUNK, PACK], BF16, name="h", align_bytes=64) for c in range(S // CHUNK)]
-        hidden(hs[0], 0)
-        nc.vector.quantize_mx(out=w2_codes[:].bitcast(FP8X4), scales=w2_plane[:], in_=w2_grouped[:].rearrange("p n j -> p (n j)"))
-        hidden(hs[0], 1)
-        light(0, 2, "result")
-        light(0, 3, "result")
-        for c in range(1, S // CHUNK):
-            hidden(hs[c], 2 * c)
-            quantize_hidden(hs[c - 1], c - 1)
-            hidden(hs[c], 2 * c + 1)
-        quantize_hidden(hs[-1], S // CHUNK - 1)
-        second(0, 0)
-        for c in range(4):
-            light(1, c, "result")
-        second(1, 0)
-        second(0, 1)
-        second(1, 1)
+        z0 = [keep.tile([P, CHUNK], F32, name=f"z0_{c}") for c in range(S // CHUNK)]
+        z1 = keep.tile([P, 2 * CHUNK], F32, name="z1")
 
-        scatter(0, 0, S // 2)
-        scatter(1, 0, S // 4)
-        scatter(0, S // 2, S)
+        def first_rows(c):
+            second(z_banks[0][:, :CHUNK], 0, c * CHUNK, (c + 1) * CHUNK)
+            scatter(0, c * CHUNK, z0[c][:], z_banks[0][:, :CHUNK])
+
+        h_first = keep.tile([P, CHUNK * PACK], BF16, name="h_first", align_bytes=64)
+        h = keep.tile([P, CHUNK * PACK], BF16, name="h", align_bytes=64)
+        hidden_on_vector(h_first, 0)
+        hidden_on_vector(h_first, 1)
+        hidden_on_vector(h, 2)
+        quantize_hidden(h_first, 0)
+        nc.vector.quantize_mx(out=w2_codes[:].bitcast(FP8X4), scales=w2_plane[:], in_=grouped["w3"][:, PACK * N :])
+        hidden_on_vector(h, 3)
+        quantize_hidden(h, 1)
+        first_rows(0)
+        hidden_on_gpsimd(h, 4)
+        first_rows(1)
+        second(z_banks[1][:], 1, 0, 2 * CHUNK)
+        hidden_on_gpsimd(h, 5)
+        light(1)
+        quantize_hidden(h, 2)
+        scatter(1, 0, ups[5][:, :CHUNK], z_banks[1][:, :CHUNK])
+        hidden_on_gpsimd(h, 6)
+        first_rows(2)
+        hidden_on_gpsimd(h, 7)
+        quantize_hidden(h, 3)
+        scatter(1, CHUNK, ups[7][:, :CHUNK], z_banks[1][:, CHUNK:])
+        first_rows(3)
         nc.sync.dma_start(out=out[0:P, :], in_=windows[0][:])
-        scatter(1, S // 4, S)
+        second(y_banks[0][:], 1, 2 * CHUNK, S)
+        scatter(1, 2 * CHUNK, z1[:], y_banks[0][:])
         nc.sync.dma_start(out=out[P : 2 * P, : T // 2], in_=windows[1][:, : T // 2])
         nc.scalar.dma_start(out=out[P : 2 * P, T // 2 :], in_=windows[1][:, T // 2 :])

@@ -23,6 +23,7 @@ BANK = 512
 GROUP = 128
 CHUNK = 256
 HALF = H // 2
+EARLY = S - CHUNK
 
 
 def load_scale_rows(nc, plane, scales):
@@ -35,13 +36,20 @@ def tile_moe_cas_glu_relu_kernel(tc, x_words, x_scales, w_words, w_scales, w1, w
     nc = tc.nc
     with ExitStack() as ctx:
         keep = ctx.enter_context(tc.tile_pool(name="keep", bufs=1))
+        reuse = ctx.enter_context(tc.tile_pool(name="reuse", bufs=1))
+        handed = ctx.enter_context(tc.tile_pool(name="handed", bufs=1))
         psum = ctx.enter_context(tc.psum_pool(name="psum", bufs=1))
 
-        def banks(name):
-            return [psum.tile([P, BANK], F32, name=f"{name}{i}") for i in range(2)]
+        def banks(name, count):
+            return [psum.tile([P, BANK], F32, name=f"{name}{i}") for i in range(count)]
 
-        sums = {"w1": banks("a1_bank"), "w3": banks("a3_bank")}
-        y_banks, z_banks = banks("y_bank"), banks("z_bank")
+        ring = banks("ring_bank", 5)
+
+        def ring_bank():
+            ring.append(ring.pop(0))
+            return ring[-1]
+
+        side = banks("side_bank", 3)
 
         offsets = keep.tile([P, S // 16], U16, name="offsets")
         x_plane = keep.tile([P, T], U8, name="x_plane", align_bytes=64)
@@ -69,16 +77,16 @@ def tile_moe_cas_glu_relu_kernel(tc, x_words, x_scales, w_words, w_scales, w1, w
         nc.sync.dma_start(out=w2_raw[:], in_=w2.rearrange("(p j) c -> p j c", j=PACK))
 
         slot_plane = keep.tile([P, S], U8, name="slot_plane", align_bytes=64)
-        slot_codes = keep.tile([P, S], U32, name="slot_codes", align_bytes=64)
+        early_codes = keep.tile([P, EARLY], U32, name="early_codes", align_bytes=64)
         nc.vector.tensor_copy(slot_plane[:], x_plane[:].indirect(offsets[:]))
-        nc.vector.tensor_copy(slot_codes[:], x_codes[:].bitcast(U32).indirect(offsets[:]))
+        nc.vector.tensor_copy(early_codes[:], x_codes[:].bitcast(U32).indirect(offsets[:, : EARLY // 16]))
 
         windows = [keep.tile([P, T], F32, name=f"window{b}") for b in range(N // P)]
 
-        def light(b):
+        def light(b, held=None):
             for c in range(T // BANK):
                 cols = slice(c * BANK, (c + 1) * BANK)
-                y = y_banks[c % 2]
+                y = side[0] if c == held else ring_bank()
                 nc.tensor.matmul_mx(
                     out=y[:],
                     lhsT=w_codes[:, 2 * P * b : 2 * P * (b + 1)].bitcast(FP4X4),
@@ -90,12 +98,12 @@ def tile_moe_cas_glu_relu_kernel(tc, x_words, x_scales, w_words, w_scales, w1, w
                 )
                 nc.scalar.copy(out=windows[b][:, cols], in_=y[:])
 
-        grouped = {name: keep.tile([P, PACK * H], BF16, name=f"{name}_grouped", align_bytes=64) for name in ("w1", "w3")}
+        grouped = {
+            "w1": keep.tile([P, PACK * H], BF16, name="w1_grouped", align_bytes=64),
+            "w3": keep.tile([P, PACK * H], BF16, name="w3_grouped", align_bytes=64),
+        }
         codes = {name: keep.tile([P, H], U32, name=f"{name}_codes", align_bytes=64) for name in ("w1", "w3")}
         plane = {name: keep.tile([P, H], U8, name=f"{name}_plane", align_bytes=64) for name in ("w1", "w3")}
-
-        def round_on_gpsimd(out, in_):
-            nc.gpsimd.tensor_scalar(out=out, in0=in_, scalar1=1.0, scalar2=0.0, op0=MULT, op1=ADD)
 
         def regroup(copy, name, half, walk="m j t"):
             m = slice(half * P // 2, (half + 1) * P // 2)
@@ -109,7 +117,7 @@ def tile_moe_cas_glu_relu_kernel(tc, x_words, x_scales, w_words, w_scales, w1, w
                 nc.vector.quantize_mx(out=codes[name][:, cols].bitcast(FP8X4), scales=plane[name][:, cols], in_=grouped[name][:, PACK * lo : PACK * (lo + step)])
 
         regroup(nc.scalar.copy, "w1", 0)
-        regroup(round_on_gpsimd, "w1", 1, "t m j")
+        regroup(nc.vector.tensor_copy, "w1", 1)
         quantize_first("w1", 1)
         regroup(nc.vector.tensor_copy, "w3", 0)
         regroup(nc.vector.tensor_copy, "w3", 1)
@@ -118,24 +126,29 @@ def tile_moe_cas_glu_relu_kernel(tc, x_words, x_scales, w_words, w_scales, w1, w
 
         w2_codes = keep.tile([P, N], U32, name="w2_codes", align_bytes=64)
         w2_plane = keep.tile([P, N], U8, name="w2_plane", align_bytes=64)
-        round_on_gpsimd(out=grouped["w3"][:, PACK * N :].rearrange("p (n j) -> p n j", j=PACK), in_=w2_raw[:].rearrange("p j n -> p n j"))
+        h_pair = keep.tile([P, 2 * CHUNK * PACK], BF16, name="h_pair", align_bytes=64)
+        w2_grouped = grouped["w3"][:, PACK * N :]
+        nc.vector.tensor_copy(out=w2_grouped.rearrange("p (c i j) -> p c j i", i=4, j=PACK), in_=w2_raw[:].rearrange("p j (c i) -> p c j i", i=4))
 
-        def first_product(name, g):
+        def first_product(name, g, acc):
             cols = slice(g * GROUP, (g + 1) * GROUP)
-            acc = sums[name][g % 2]
+            first = max(k for k in slot_codes if k <= g * GROUP)
+            words = slot_codes[first][:, g * GROUP - first : (g + 1) * GROUP - first]
             for t in range(PACK):
                 nc.tensor.matmul_mx(
                     out=acc[:, t * GROUP : (t + 1) * GROUP],
                     lhsT=codes[name][:, t * P : (t + 1) * P].bitcast(FP8X4),
                     lhsT_scale=plane[name][:, t * P : (t + 1) * P],
-                    rhs=slot_codes[:, cols].bitcast(FP8X4),
+                    rhs=words.bitcast(FP8X4),
                     rhs_scale=slot_plane[:, cols],
                     start=True,
                     stop=True,
                 )
             return acc[:].rearrange("p (t s) -> p s t", t=PACK)
 
-        gates = [keep.tile([P, GROUP * PACK], F32, name=f"gate{g}") for g in range(S // GROUP)]
+        gates = {g: keep.tile([P, GROUP * PACK], F32, name=f"gate{g}")[:] for g in range(S // GROUP) if g != 1}
+        gates[1] = reuse.tile([P, GROUP * PACK], F32, name="gate1", align_bytes=64, offset=0)[:]
+        slot_codes = {0: early_codes}
         ups = {g: keep.tile([P, GROUP * PACK], F32, name=f"up{g}") for g in range(4, S // GROUP)}
 
         def by_slot(ap):
@@ -146,27 +159,30 @@ def tile_moe_cas_glu_relu_kernel(tc, x_words, x_scales, w_words, w_scales, w1, w
             return h[:, lo : lo + GROUP * PACK]
 
         def hidden_on_vector(h, g):
-            nc.scalar.activation(out=by_slot(gates[g][:]), in_=first_product("w1", g), func=RELU)
-            nc.vector.tensor_tensor(out=by_slot(part(h, g)), in0=first_product("w3", g), in1=by_slot(gates[g][:]), op=MULT)
+            nc.scalar.activation(out=by_slot(gates[g]), in_=first_product("w1", g, ring_bank()), func=RELU)
+            nc.vector.tensor_tensor(out=by_slot(part(h, g)), in0=first_product("w3", g, side[g % 3]), in1=by_slot(gates[g]), op=MULT)
 
-        def hidden_on_gpsimd(h, g):
-            nc.scalar.activation(out=by_slot(gates[g][:]), in_=first_product("w1", g), func=RELU)
-            nc.scalar.copy(out=by_slot(ups[g][:]), in_=first_product("w3", g))
-            nc.gpsimd.tensor_tensor(out=part(h, g), in0=ups[g][:], in1=gates[g][:], op=MULT)
+        def hidden_on_gpsimd(h, g, a1_bank, a3_bank):
+            nc.scalar.copy(out=by_slot(ups[g][:]), in_=first_product("w3", g, a3_bank))
+            nc.scalar.activation(out=by_slot(gates[g]), in_=first_product("w1", g, a1_bank), func=RELU)
+            nc.gpsimd.tensor_tensor(out=part(h, g), in0=ups[g][:], in1=gates[g], op=MULT)
 
-        h_codes = keep.tile([P, S], U32, name="h_codes", align_bytes=64)
+        h_codes = {0: keep.tile([P, CHUNK], U32, name="h_codes", align_bytes=64)}
         h_plane = keep.tile([P, S], U8, name="h_plane", align_bytes=64)
 
-        def quantize_hidden(h, c):
-            cols = slice(c * CHUNK, (c + 1) * CHUNK)
-            nc.vector.quantize_mx(out=h_codes[:, cols].bitcast(FP8X4), scales=h_plane[:, cols], in_=h[:])
+        def h_words(lo, hi):
+            first = max(k for k in h_codes if k <= lo)
+            return h_codes[first][:, lo - first : hi - first].bitcast(FP8X4)
+
+        def quantize_hidden(h, lo, hi):
+            nc.vector.quantize_mx(out=h_words(lo, hi), scales=h_plane[:, lo:hi], in_=h)
 
         def second(acc, b, lo, hi):
             nc.tensor.matmul_mx(
                 out=acc,
                 lhsT=w2_codes[:, b * P : (b + 1) * P].bitcast(FP8X4),
                 lhsT_scale=w2_plane[:, b * P : (b + 1) * P],
-                rhs=h_codes[:, lo:hi].bitcast(FP8X4),
+                rhs=h_words(lo, hi),
                 rhs_scale=h_plane[:, lo:hi],
                 start=True,
                 stop=True,
@@ -176,38 +192,41 @@ def tile_moe_cas_glu_relu_kernel(tc, x_words, x_scales, w_words, w_scales, w1, w
             nc.scalar.copy(out=z, in_=acc)
             nc.vector.tensor_copy(windows[b][:].indirect(offsets[:, lo // 16 : (lo + z.shape[1]) // 16]), z)
 
-        z0 = [keep.tile([P, CHUNK], F32, name=f"z0_{c}") for c in range(S // CHUNK)]
+        def rows(b, lo, hi, z, bank):
+            second(bank[:, : hi - lo], b, lo, hi)
+            scatter(b, lo, z, bank[:, : hi - lo])
+
+        z_first = handed.tile([P, CHUNK], F32, name="z_first", align_bytes=64, offset=8 * CHUNK)
+        z_last = keep.tile([P, CHUNK], F32, name="z_last")
         z1 = keep.tile([P, 2 * CHUNK], F32, name="z1")
+        h_low, h_high = h_pair[:, : CHUNK * PACK], h_pair[:, CHUNK * PACK :]
 
-        def first_rows(c):
-            second(z_banks[0][:, :CHUNK], 0, c * CHUNK, (c + 1) * CHUNK)
-            scatter(0, c * CHUNK, z0[c][:], z_banks[0][:, :CHUNK])
-
-        h_first = keep.tile([P, CHUNK * PACK], BF16, name="h_first", align_bytes=64)
-        h = keep.tile([P, CHUNK * PACK], BF16, name="h", align_bytes=64)
-        hidden_on_vector(h_first, 0)
-        hidden_on_vector(h_first, 1)
-        hidden_on_vector(h, 2)
-        quantize_hidden(h_first, 0)
-        nc.vector.quantize_mx(out=w2_codes[:].bitcast(FP8X4), scales=w2_plane[:], in_=grouped["w3"][:, PACK * N :])
-        hidden_on_vector(h, 3)
-        quantize_hidden(h, 1)
-        first_rows(0)
-        hidden_on_gpsimd(h, 4)
-        first_rows(1)
-        second(z_banks[1][:], 1, 0, 2 * CHUNK)
-        hidden_on_gpsimd(h, 5)
-        light(1)
-        quantize_hidden(h, 2)
-        scatter(1, 0, ups[5][:, :CHUNK], z_banks[1][:, :CHUNK])
-        hidden_on_gpsimd(h, 6)
-        first_rows(2)
-        hidden_on_gpsimd(h, 7)
-        quantize_hidden(h, 3)
-        scatter(1, CHUNK, ups[7][:, :CHUNK], z_banks[1][:, CHUNK:])
-        first_rows(3)
+        hidden_on_vector(h_high, 0)
+        hidden_on_vector(h_high, 1)
+        nc.vector.quantize_mx(out=w2_codes[:].bitcast(FP8X4), scales=w2_plane[:], in_=w2_grouped)
+        quantize_hidden(h_high, 0, CHUNK)
+        hidden_on_vector(h_low, 2)
+        hidden_on_vector(h_low, 3)
+        slot_codes[EARLY] = reuse.tile([P, S - EARLY], U32, name="late_codes", align_bytes=64, offset=0)
+        nc.vector.tensor_copy(slot_codes[EARLY][:], x_codes[:].bitcast(U32).indirect(offsets[:, EARLY // 16 :]))
+        hidden_on_gpsimd(h_high, 4, ring_bank(), ring_bank())
+        rows(0, 0, CHUNK, z_first[:], ring_bank())
+        hidden_on_gpsimd(h_high, 5, ring_bank(), ring_bank())
+        light(1, held=2)
+        h_codes[CHUNK] = handed.tile([P, 2 * CHUNK], U32, name="h_codes_pair", align_bytes=64, offset=8 * CHUNK)
+        quantize_hidden(h_pair[:], CHUNK, EARLY)
+        rows(1, 0, CHUNK, ups[5][:, :CHUNK], side[0])
+        z_pair = handed.tile([P, 2 * CHUNK], F32, name="z_pair", align_bytes=64, offset=0)
+        hidden_on_gpsimd(h_low, 6, ring_bank(), ring_bank())
+        rows(0, CHUNK, EARLY, z_pair[:], ring_bank())
+        hidden_on_gpsimd(h_low, 7, ring_bank(), ring_bank())
+        h_codes[EARLY] = handed.tile([P, CHUNK], U32, name="h_codes_late", align_bytes=64, offset=0)
+        quantize_hidden(h_low, EARLY, S)
+        rows(1, CHUNK, 2 * CHUNK, ups[7][:, :CHUNK], side[1])
+        rows(0, EARLY, S, z_last[:], ring_bank())
         nc.sync.dma_start(out=out[0:P, :], in_=windows[0][:])
-        second(y_banks[0][:], 1, 2 * CHUNK, S)
-        scatter(1, 2 * CHUNK, z1[:], y_banks[0][:])
+        second(side[2][:, :CHUNK], 1, 2 * CHUNK, EARLY)
+        second(side[2][:, CHUNK:], 1, EARLY, S)
+        scatter(1, 2 * CHUNK, z1[:], side[2][:])
         nc.sync.dma_start(out=out[P : 2 * P, : T // 2], in_=windows[1][:, : T // 2])
         nc.scalar.dma_start(out=out[P : 2 * P, T // 2 :], in_=windows[1][:, T // 2 :])

@@ -15,15 +15,18 @@ FP8X4 = mybir.dt.float8_e4m3fn_x4
 FP4X4 = mybir.dt.float4_e2m1fn_x4
 RELU = mybir.ActivationFunctionType.Relu
 MULT = mybir.AluOpType.mult
-ADD = mybir.AluOpType.add
 
 P = 128
 PACK = 4
 BANK = 512
-GROUP = 128
-CHUNK = 256
+GROUP = BANK // PACK
+GROUPS = S // GROUP
+CHUNK = 2 * GROUP
+ON_VECTOR = GROUPS // 2
 HALF = H // 2
 EARLY = S - CHUNK
+RING_BANKS = 5
+SIDE_BANKS = 3
 
 
 def load_scale_rows(nc, plane, scales):
@@ -36,20 +39,16 @@ def tile_moe_cas_glu_relu_kernel(tc, x_words, x_scales, w_words, w_scales, w1, w
     nc = tc.nc
     with ExitStack() as ctx:
         keep = ctx.enter_context(tc.tile_pool(name="keep", bufs=1))
-        reuse = ctx.enter_context(tc.tile_pool(name="reuse", bufs=1))
-        handed = ctx.enter_context(tc.tile_pool(name="handed", bufs=1))
+        after_gate = ctx.enter_context(tc.tile_pool(name="after_gate", bufs=1))
+        after_result = ctx.enter_context(tc.tile_pool(name="after_result", bufs=1))
         psum = ctx.enter_context(tc.psum_pool(name="psum", bufs=1))
 
-        def banks(name, count):
-            return [psum.tile([P, BANK], F32, name=f"{name}{i}") for i in range(count)]
-
-        ring = banks("ring_bank", 5)
+        ring = [psum.tile([P, BANK], F32, name=f"ring_bank{i}") for i in range(RING_BANKS)]
+        side = [psum.tile([P, BANK], F32, name=f"side_bank{i}") for i in range(SIDE_BANKS)]
 
         def ring_bank():
             ring.append(ring.pop(0))
             return ring[-1]
-
-        side = banks("side_bank", 3)
 
         offsets = keep.tile([P, S // 16], U16, name="offsets")
         x_plane = keep.tile([P, T], U8, name="x_plane", align_bytes=64)
@@ -77,16 +76,19 @@ def tile_moe_cas_glu_relu_kernel(tc, x_words, x_scales, w_words, w_scales, w1, w
         nc.sync.dma_start(out=w2_raw[:], in_=w2.rearrange("(p j) c -> p j c", j=PACK))
 
         slot_plane = keep.tile([P, S], U8, name="slot_plane", align_bytes=64)
-        early_codes = keep.tile([P, EARLY], U32, name="early_codes", align_bytes=64)
+        slot_codes = {0: keep.tile([P, EARLY], U32, name="early_codes", align_bytes=64)}
         nc.vector.tensor_copy(slot_plane[:], x_plane[:].indirect(offsets[:]))
-        nc.vector.tensor_copy(early_codes[:], x_codes[:].bitcast(U32).indirect(offsets[:, : EARLY // 16]))
+        nc.vector.tensor_copy(slot_codes[0][:], x_codes[:].bitcast(U32).indirect(offsets[:, : EARLY // 16]))
+
+        def words(tiles, lo, hi):
+            first = max(k for k in tiles if k <= lo)
+            return tiles[first][:, lo - first : hi - first].bitcast(FP8X4)
 
         windows = [keep.tile([P, T], F32, name=f"window{b}") for b in range(N // P)]
 
-        def light(b, held=None):
-            for c in range(T // BANK):
+        def light(b, y_banks):
+            for c, y in enumerate(y_banks):
                 cols = slice(c * BANK, (c + 1) * BANK)
-                y = side[0] if c == held else ring_bank()
                 nc.tensor.matmul_mx(
                     out=y[:],
                     lhsT=w_codes[:, 2 * P * b : 2 * P * (b + 1)].bitcast(FP4X4),
@@ -98,17 +100,14 @@ def tile_moe_cas_glu_relu_kernel(tc, x_words, x_scales, w_words, w_scales, w1, w
                 )
                 nc.scalar.copy(out=windows[b][:, cols], in_=y[:])
 
-        grouped = {
-            "w1": keep.tile([P, PACK * H], BF16, name="w1_grouped", align_bytes=64),
-            "w3": keep.tile([P, PACK * H], BF16, name="w3_grouped", align_bytes=64),
-        }
+        grouped = {name: keep.tile([P, PACK * H], BF16, name=f"{name}_grouped", align_bytes=64) for name in ("w1", "w3")}
         codes = {name: keep.tile([P, H], U32, name=f"{name}_codes", align_bytes=64) for name in ("w1", "w3")}
         plane = {name: keep.tile([P, H], U8, name=f"{name}_plane", align_bytes=64) for name in ("w1", "w3")}
 
-        def regroup(copy, name, half, walk="m j t"):
+        def regroup(copy, name, half):
             m = slice(half * P // 2, (half + 1) * P // 2)
             whole = grouped[name][:].rearrange("p (t m j) -> p t m j", t=PACK, j=PACK)
-            copy(out=whole[:, :, m, :].rearrange(f"p t m j -> p {walk}"), in_=raw[name, half][:].rearrange(f"p j (m t) -> p {walk}", t=PACK))
+            copy(out=whole[:, :, m, :].rearrange("p t m j -> p m j t"), in_=raw[name, half][:].rearrange("p j (m t) -> p m j t", t=PACK))
 
         def quantize_first(name, pieces):
             step = H // pieces
@@ -121,8 +120,8 @@ def tile_moe_cas_glu_relu_kernel(tc, x_words, x_scales, w_words, w_scales, w1, w
         quantize_first("w1", 1)
         regroup(nc.vector.tensor_copy, "w3", 0)
         regroup(nc.vector.tensor_copy, "w3", 1)
-        quantize_first("w3", 4)
-        light(0)
+        quantize_first("w3", PACK)
+        light(0, [ring_bank() for c in range(T // BANK)])
 
         w2_codes = keep.tile([P, N], U32, name="w2_codes", align_bytes=64)
         w2_plane = keep.tile([P, N], U8, name="w2_plane", align_bytes=64)
@@ -131,25 +130,22 @@ def tile_moe_cas_glu_relu_kernel(tc, x_words, x_scales, w_words, w_scales, w1, w
         nc.vector.tensor_copy(out=w2_grouped.rearrange("p (c i j) -> p c j i", i=4, j=PACK), in_=w2_raw[:].rearrange("p j (c i) -> p c j i", i=4))
 
         def first_product(name, g, acc):
-            cols = slice(g * GROUP, (g + 1) * GROUP)
-            first = max(k for k in slot_codes if k <= g * GROUP)
-            words = slot_codes[first][:, g * GROUP - first : (g + 1) * GROUP - first]
             for t in range(PACK):
                 nc.tensor.matmul_mx(
                     out=acc[:, t * GROUP : (t + 1) * GROUP],
                     lhsT=codes[name][:, t * P : (t + 1) * P].bitcast(FP8X4),
                     lhsT_scale=plane[name][:, t * P : (t + 1) * P],
-                    rhs=words.bitcast(FP8X4),
-                    rhs_scale=slot_plane[:, cols],
+                    rhs=words(slot_codes, g * GROUP, (g + 1) * GROUP),
+                    rhs_scale=slot_plane[:, g * GROUP : (g + 1) * GROUP],
                     start=True,
                     stop=True,
                 )
             return acc[:].rearrange("p (t s) -> p s t", t=PACK)
 
-        gates = {g: keep.tile([P, GROUP * PACK], F32, name=f"gate{g}")[:] for g in range(S // GROUP) if g != 1}
-        gates[1] = reuse.tile([P, GROUP * PACK], F32, name="gate1", align_bytes=64, offset=0)[:]
-        slot_codes = {0: early_codes}
-        ups = {g: keep.tile([P, GROUP * PACK], F32, name=f"up{g}") for g in range(4, S // GROUP)}
+        handed_on = CHUNK // GROUP - 1
+        gates = {g: keep.tile([P, GROUP * PACK], F32, name=f"gate{g}") for g in range(GROUPS) if g != handed_on}
+        gates[handed_on] = after_gate.tile([P, GROUP * PACK], F32, name="handed_gate", align_bytes=64, offset=0)
+        ups = {g: keep.tile([P, GROUP * PACK], F32, name=f"up{g}") for g in range(ON_VECTOR, GROUPS)}
 
         def by_slot(ap):
             return ap.rearrange("p (s t) -> p s t", t=PACK)
@@ -159,30 +155,26 @@ def tile_moe_cas_glu_relu_kernel(tc, x_words, x_scales, w_words, w_scales, w1, w
             return h[:, lo : lo + GROUP * PACK]
 
         def hidden_on_vector(h, g):
-            nc.scalar.activation(out=by_slot(gates[g]), in_=first_product("w1", g, ring_bank()), func=RELU)
-            nc.vector.tensor_tensor(out=by_slot(part(h, g)), in0=first_product("w3", g, side[g % 3]), in1=by_slot(gates[g]), op=MULT)
+            nc.scalar.activation(out=by_slot(gates[g][:]), in_=first_product("w1", g, ring_bank()), func=RELU)
+            nc.vector.tensor_tensor(out=by_slot(part(h, g)), in0=first_product("w3", g, side[g % SIDE_BANKS]), in1=by_slot(gates[g][:]), op=MULT)
 
         def hidden_on_gpsimd(h, g, a1_bank, a3_bank):
             nc.scalar.copy(out=by_slot(ups[g][:]), in_=first_product("w3", g, a3_bank))
-            nc.scalar.activation(out=by_slot(gates[g]), in_=first_product("w1", g, a1_bank), func=RELU)
-            nc.gpsimd.tensor_tensor(out=part(h, g), in0=ups[g][:], in1=gates[g], op=MULT)
+            nc.scalar.activation(out=by_slot(gates[g][:]), in_=first_product("w1", g, a1_bank), func=RELU)
+            nc.gpsimd.tensor_tensor(out=part(h, g), in0=ups[g][:], in1=gates[g][:], op=MULT)
 
-        h_codes = {0: keep.tile([P, CHUNK], U32, name="h_codes", align_bytes=64)}
+        h_codes = {0: keep.tile([P, CHUNK], U32, name="h_codes_first", align_bytes=64)}
         h_plane = keep.tile([P, S], U8, name="h_plane", align_bytes=64)
 
-        def h_words(lo, hi):
-            first = max(k for k in h_codes if k <= lo)
-            return h_codes[first][:, lo - first : hi - first].bitcast(FP8X4)
-
         def quantize_hidden(h, lo, hi):
-            nc.vector.quantize_mx(out=h_words(lo, hi), scales=h_plane[:, lo:hi], in_=h)
+            nc.vector.quantize_mx(out=words(h_codes, lo, hi), scales=h_plane[:, lo:hi], in_=h)
 
-        def second(acc, b, lo, hi):
+        def second_product(acc, b, lo, hi):
             nc.tensor.matmul_mx(
                 out=acc,
                 lhsT=w2_codes[:, b * P : (b + 1) * P].bitcast(FP8X4),
                 lhsT_scale=w2_plane[:, b * P : (b + 1) * P],
-                rhs=h_words(lo, hi),
+                rhs=words(h_codes, lo, hi),
                 rhs_scale=h_plane[:, lo:hi],
                 start=True,
                 stop=True,
@@ -192,13 +184,13 @@ def tile_moe_cas_glu_relu_kernel(tc, x_words, x_scales, w_words, w_scales, w1, w
             nc.scalar.copy(out=z, in_=acc)
             nc.vector.tensor_copy(windows[b][:].indirect(offsets[:, lo // 16 : (lo + z.shape[1]) // 16]), z)
 
-        def rows(b, lo, hi, z, bank):
-            second(bank[:, : hi - lo], b, lo, hi)
+        def results(b, lo, hi, z, bank):
+            second_product(bank[:, : hi - lo], b, lo, hi)
             scatter(b, lo, z, bank[:, : hi - lo])
 
-        z_first = handed.tile([P, CHUNK], F32, name="z_first", align_bytes=64, offset=8 * CHUNK)
+        z_first = after_result.tile([P, CHUNK], F32, name="z_first", align_bytes=64, offset=0)
         z_last = keep.tile([P, CHUNK], F32, name="z_last")
-        z1 = keep.tile([P, 2 * CHUNK], F32, name="z1")
+        z_end = keep.tile([P, 2 * CHUNK], F32, name="z_end")
         h_low, h_high = h_pair[:, : CHUNK * PACK], h_pair[:, CHUNK * PACK :]
 
         hidden_on_vector(h_high, 0)
@@ -207,26 +199,29 @@ def tile_moe_cas_glu_relu_kernel(tc, x_words, x_scales, w_words, w_scales, w1, w
         quantize_hidden(h_high, 0, CHUNK)
         hidden_on_vector(h_low, 2)
         hidden_on_vector(h_low, 3)
-        slot_codes[EARLY] = reuse.tile([P, S - EARLY], U32, name="late_codes", align_bytes=64, offset=0)
+        slot_codes[EARLY] = after_gate.tile([P, S - EARLY], U32, name="late_codes", align_bytes=64, offset=0)
         nc.vector.tensor_copy(slot_codes[EARLY][:], x_codes[:].bitcast(U32).indirect(offsets[:, EARLY // 16 :]))
+
         hidden_on_gpsimd(h_high, 4, ring_bank(), ring_bank())
-        rows(0, 0, CHUNK, z_first[:], ring_bank())
+        results(0, 0, CHUNK, z_first[:], ring_bank())
         hidden_on_gpsimd(h_high, 5, ring_bank(), ring_bank())
-        light(1, held=2)
-        h_codes[CHUNK] = handed.tile([P, 2 * CHUNK], U32, name="h_codes_pair", align_bytes=64, offset=8 * CHUNK)
+        light(1, [ring_bank(), ring_bank(), side[0], ring_bank()])
+        h_codes[CHUNK] = after_result.tile([P, 2 * CHUNK], U32, name="h_codes_pair", align_bytes=64, offset=0)
         quantize_hidden(h_pair[:], CHUNK, EARLY)
-        rows(1, 0, CHUNK, ups[5][:, :CHUNK], side[0])
-        z_pair = handed.tile([P, 2 * CHUNK], F32, name="z_pair", align_bytes=64, offset=0)
+
+        results(1, 0, CHUNK, ups[5][:, :CHUNK], side[0])
+        z_pair = keep.tile([P, 2 * CHUNK], F32, name="z_pair")
         hidden_on_gpsimd(h_low, 6, ring_bank(), ring_bank())
-        rows(0, CHUNK, EARLY, z_pair[:], ring_bank())
-        hidden_on_gpsimd(h_low, 7, ring_bank(), ring_bank())
-        h_codes[EARLY] = handed.tile([P, CHUNK], U32, name="h_codes_late", align_bytes=64, offset=0)
+        results(0, CHUNK, EARLY, z_pair[:], ring_bank())
+        hidden_on_gpsimd(h_low, 7, ring[-1], ring_bank())
+        h_codes[EARLY] = keep.tile([P, CHUNK], U32, name="h_codes_last", align_bytes=64)
         quantize_hidden(h_low, EARLY, S)
-        rows(1, CHUNK, 2 * CHUNK, ups[7][:, :CHUNK], side[1])
-        rows(0, EARLY, S, z_last[:], ring_bank())
+        results(1, CHUNK, 2 * CHUNK, ups[7][:, :CHUNK], side[1])
+
+        results(0, EARLY, S, z_last[:], ring_bank())
         nc.sync.dma_start(out=out[0:P, :], in_=windows[0][:])
-        second(side[2][:, :CHUNK], 1, 2 * CHUNK, EARLY)
-        second(side[2][:, CHUNK:], 1, EARLY, S)
-        scatter(1, 2 * CHUNK, z1[:], side[2][:])
+        second_product(side[2][:, :CHUNK], 1, 2 * CHUNK, EARLY)
+        second_product(side[2][:, CHUNK:], 1, EARLY, S)
+        scatter(1, 2 * CHUNK, z_end[:], side[2][:])
         nc.sync.dma_start(out=out[P : 2 * P, : T // 2], in_=windows[1][:, : T // 2])
         nc.scalar.dma_start(out=out[P : 2 * P, T // 2 :], in_=windows[1][:, T // 2 :])

@@ -15,6 +15,7 @@ FP8X4 = mybir.dt.float8_e4m3fn_x4
 FP4X4 = mybir.dt.float4_e2m1fn_x4
 RELU = mybir.ActivationFunctionType.Relu
 MULT = mybir.AluOpType.mult
+ADD = mybir.AluOpType.add
 
 P = 128
 PACK = 4
@@ -25,8 +26,6 @@ CHUNK = 2 * GROUP
 ON_VECTOR = GROUPS // 2
 HALF = H // 2
 EARLY = S - CHUNK
-RING_BANKS = 5
-SIDE_BANKS = 3
 
 
 def load_scale_rows(nc, plane, scales):
@@ -43,12 +42,7 @@ def tile_moe_cas_glu_relu_kernel(tc, x_words, x_scales, w_words, w_scales, w1, w
         after_result = ctx.enter_context(tc.tile_pool(name="after_result", bufs=1))
         psum = ctx.enter_context(tc.psum_pool(name="psum", bufs=1))
 
-        ring = [psum.tile([P, BANK], F32, name=f"ring_bank{i}") for i in range(RING_BANKS)]
-        side = [psum.tile([P, BANK], F32, name=f"side_bank{i}") for i in range(SIDE_BANKS)]
-
-        def ring_bank():
-            ring.append(ring.pop(0))
-            return ring[-1]
+        bank = [psum.tile([P, BANK], F32, name=f"bank{i}") for i in range(8)]
 
         offsets = keep.tile([P, S // 16], U16, name="offsets")
         x_plane = keep.tile([P, T], U8, name="x_plane", align_bytes=64)
@@ -58,7 +52,8 @@ def tile_moe_cas_glu_relu_kernel(tc, x_words, x_scales, w_words, w_scales, w1, w
         nc.vector.memset(x_plane[:].bitcast(I32), 0)
         nc.vector.memset(w_plane[:].bitcast(I32), 0)
 
-        raw = {(name, half): keep.tile([P, PACK, HALF], F32, name=f"{name}_raw{half}") for name in ("w1", "w3") for half in range(2)}
+        raw = {(name, half): keep.tile([P, PACK, HALF], F32, name=f"{name}_raw{half}") for name, half in (("w1", 0), ("w1", 1), ("w3", 0))}
+        raw["w3", 1] = after_gate.tile([P, PACK, HALF], F32, name="w3_raw1", align_bytes=64, offset=0)
         w2_raw = keep.tile([P, PACK, N], F32, name="w2_raw")
 
         def load_half(name, w, half):
@@ -86,8 +81,8 @@ def tile_moe_cas_glu_relu_kernel(tc, x_words, x_scales, w_words, w_scales, w1, w
 
         windows = [keep.tile([P, T], F32, name=f"window{b}") for b in range(N // P)]
 
-        def light(b, y_banks):
-            for c, y in enumerate(y_banks):
+        def light(b, first, y_banks):
+            for c, y in enumerate(y_banks, first):
                 cols = slice(c * BANK, (c + 1) * BANK)
                 nc.tensor.matmul_mx(
                     out=y[:],
@@ -111,7 +106,7 @@ def tile_moe_cas_glu_relu_kernel(tc, x_words, x_scales, w_words, w_scales, w1, w
 
         def quantize_first(name, pieces):
             step = H // pieces
-            for lo in range(0, H, step):
+            for lo in reversed(range(0, H, step)):
                 cols = slice(lo, lo + step)
                 nc.vector.quantize_mx(out=codes[name][:, cols].bitcast(FP8X4), scales=plane[name][:, cols], in_=grouped[name][:, PACK * lo : PACK * (lo + step)])
 
@@ -121,16 +116,19 @@ def tile_moe_cas_glu_relu_kernel(tc, x_words, x_scales, w_words, w_scales, w1, w
         regroup(nc.vector.tensor_copy, "w3", 0)
         regroup(nc.vector.tensor_copy, "w3", 1)
         quantize_first("w3", PACK)
-        light(0, [ring_bank() for c in range(T // BANK)])
+        light(0, 0, bank[:4])
+        light(1, 0, bank[4:5])
 
         w2_codes = keep.tile([P, N], U32, name="w2_codes", align_bytes=64)
         w2_plane = keep.tile([P, N], U8, name="w2_plane", align_bytes=64)
-        h_pair = keep.tile([P, 2 * CHUNK * PACK], BF16, name="h_pair", align_bytes=64)
-        w2_grouped = grouped["w3"][:, PACK * N :]
-        nc.vector.tensor_copy(out=w2_grouped.rearrange("p (c i j) -> p c j i", i=4, j=PACK), in_=w2_raw[:].rearrange("p j (c i) -> p c j i", i=4))
+        h_pair = grouped["w3"]
+        w2_grouped = h_pair[:, : PACK * N]
+        slot_codes[EARLY] = after_gate.tile([P, S - EARLY], U32, name="late_codes", align_bytes=64, offset=0)
+        nc.vector.tensor_copy(slot_codes[EARLY][:], x_codes[:].bitcast(U32).indirect(offsets[:, EARLY // 16 :]))
+        nc.gpsimd.tensor_scalar(w2_grouped.rearrange("p (c j) -> p c j", j=PACK), w2_raw[:].rearrange("p j c -> p c j"), 1.0, 0.0, MULT, ADD)
 
         def first_product(name, g, acc):
-            for t in range(PACK):
+            for t in reversed(range(PACK)):
                 nc.tensor.matmul_mx(
                     out=acc[:, t * GROUP : (t + 1) * GROUP],
                     lhsT=codes[name][:, t * P : (t + 1) * P].bitcast(FP8X4),
@@ -142,10 +140,9 @@ def tile_moe_cas_glu_relu_kernel(tc, x_words, x_scales, w_words, w_scales, w1, w
                 )
             return acc[:].rearrange("p (t s) -> p s t", t=PACK)
 
-        handed_on = CHUNK // GROUP - 1
-        gates = {g: keep.tile([P, GROUP * PACK], F32, name=f"gate{g}") for g in range(GROUPS) if g != handed_on}
-        gates[handed_on] = after_gate.tile([P, GROUP * PACK], F32, name="handed_gate", align_bytes=64, offset=0)
-        ups = {g: keep.tile([P, GROUP * PACK], F32, name=f"up{g}") for g in range(ON_VECTOR, GROUPS)}
+        gates = {g: keep.tile([P, GROUP * PACK], F32, name=f"gate{g}") for g in range(GROUPS)}
+        ups = {g: keep.tile([P, GROUP * PACK], F32, name=f"up{g}") for g in range(ON_VECTOR, GROUPS) if g != 5}
+        ups[5] = gates[2]
 
         def by_slot(ap):
             return ap.rearrange("p (s t) -> p s t", t=PACK)
@@ -154,13 +151,16 @@ def tile_moe_cas_glu_relu_kernel(tc, x_words, x_scales, w_words, w_scales, w1, w
             lo = g % (CHUNK // GROUP) * GROUP * PACK
             return h[:, lo : lo + GROUP * PACK]
 
-        def hidden_on_vector(h, g):
-            nc.scalar.activation(out=by_slot(gates[g][:]), in_=first_product("w1", g, ring_bank()), func=RELU)
-            nc.vector.tensor_tensor(out=by_slot(part(h, g)), in0=first_product("w3", g, side[g % SIDE_BANKS]), in1=by_slot(gates[g][:]), op=MULT)
+        def gate(g, acc):
+            nc.scalar.activation(out=by_slot(gates[g][:]), in_=first_product("w1", g, acc), func=RELU)
 
-        def hidden_on_gpsimd(h, g, a1_bank, a3_bank):
-            nc.scalar.copy(out=by_slot(ups[g][:]), in_=first_product("w3", g, a3_bank))
-            nc.scalar.activation(out=by_slot(gates[g][:]), in_=first_product("w1", g, a1_bank), func=RELU)
+        def hidden_on_vector(h, g, acc):
+            nc.vector.tensor_tensor(out=by_slot(part(h, g)), in0=first_product("w3", g, acc), in1=by_slot(gates[g][:]), op=MULT)
+
+        def stage_up(g, acc):
+            nc.scalar.copy(out=by_slot(ups[g][:]), in_=first_product("w3", g, acc))
+
+        def hidden_on_gpsimd(h, g):
             nc.gpsimd.tensor_tensor(out=part(h, g), in0=ups[g][:], in1=gates[g][:], op=MULT)
 
         h_codes = {0: keep.tile([P, CHUNK], U32, name="h_codes_first", align_bytes=64)}
@@ -193,35 +193,44 @@ def tile_moe_cas_glu_relu_kernel(tc, x_words, x_scales, w_words, w_scales, w1, w
         z_end = keep.tile([P, 2 * CHUNK], F32, name="z_end")
         h_low, h_high = h_pair[:, : CHUNK * PACK], h_pair[:, CHUNK * PACK :]
 
-        hidden_on_vector(h_high, 0)
-        hidden_on_vector(h_high, 1)
+        gate(0, bank[0])
+        gate(1, bank[1])
+        hidden_on_vector(h_high, 0, bank[6])
+        hidden_on_vector(h_high, 1, bank[7])
         nc.vector.quantize_mx(out=w2_codes[:].bitcast(FP8X4), scales=w2_plane[:], in_=w2_grouped)
         quantize_hidden(h_high, 0, CHUNK)
-        hidden_on_vector(h_low, 2)
-        hidden_on_vector(h_low, 3)
-        slot_codes[EARLY] = after_gate.tile([P, S - EARLY], U32, name="late_codes", align_bytes=64, offset=0)
-        nc.vector.tensor_copy(slot_codes[EARLY][:], x_codes[:].bitcast(U32).indirect(offsets[:, EARLY // 16 :]))
-
-        hidden_on_gpsimd(h_high, 4, ring_bank(), ring_bank())
-        results(0, 0, CHUNK, z_first[:], ring_bank())
-        hidden_on_gpsimd(h_high, 5, ring_bank(), ring_bank())
-        light(1, [ring_bank(), ring_bank(), side[0], ring_bank()])
+        gate(2, bank[2])
+        gate(3, bank[3])
+        gate(4, bank[5])
+        hidden_on_vector(h_low, 2, bank[6])
+        stage_up(4, bank[0])
+        hidden_on_gpsimd(h_high, 4)
+        gate(5, bank[4])
+        hidden_on_vector(h_low, 3, bank[7])
+        results(0, 0, CHUNK, z_first[:], bank[5])
+        stage_up(5, bank[1])
+        hidden_on_gpsimd(h_high, 5)
+        light(1, 1, [bank[6], bank[5], bank[7]])
         h_codes[CHUNK] = after_result.tile([P, 2 * CHUNK], U32, name="h_codes_pair", align_bytes=64, offset=0)
         quantize_hidden(h_pair[:], CHUNK, EARLY)
 
-        results(1, 0, CHUNK, ups[5][:, :CHUNK], side[0])
+        results(1, 0, CHUNK, ups[5][:, :CHUNK], bank[2])
         z_pair = keep.tile([P, 2 * CHUNK], F32, name="z_pair")
-        hidden_on_gpsimd(h_low, 6, ring_bank(), ring_bank())
-        results(0, CHUNK, EARLY, z_pair[:], ring_bank())
-        hidden_on_gpsimd(h_low, 7, ring[-1], ring_bank())
+        gate(6, bank[6])
+        results(0, CHUNK, EARLY, z_pair[:], bank[3])
+        stage_up(6, bank[5])
+        hidden_on_gpsimd(h_low, 6)
+        stage_up(7, bank[7])
+        gate(7, bank[3])
+        hidden_on_gpsimd(h_low, 7)
         h_codes[EARLY] = keep.tile([P, CHUNK], U32, name="h_codes_last", align_bytes=64)
         quantize_hidden(h_low, EARLY, S)
-        results(1, CHUNK, 2 * CHUNK, ups[7][:, :CHUNK], side[1])
+        results(1, CHUNK, 2 * CHUNK, ups[7][:, :CHUNK], bank[4])
 
-        results(0, EARLY, S, z_last[:], ring_bank())
+        results(0, EARLY, S, z_last[:], bank[0])
         nc.sync.dma_start(out=out[0:P, :], in_=windows[0][:])
-        second_product(side[2][:, :CHUNK], 1, 2 * CHUNK, EARLY)
-        second_product(side[2][:, CHUNK:], 1, EARLY, S)
-        scatter(1, 2 * CHUNK, z_end[:], side[2][:])
+        second_product(bank[1][:, :CHUNK], 1, 2 * CHUNK, EARLY)
+        second_product(bank[1][:, CHUNK:], 1, EARLY, S)
+        scatter(1, 2 * CHUNK, z_end[:], bank[1][:])
         nc.sync.dma_start(out=out[P : 2 * P, : T // 2], in_=windows[1][:, : T // 2])
         nc.scalar.dma_start(out=out[P : 2 * P, T // 2 :], in_=windows[1][:, T // 2 :])

@@ -208,13 +208,17 @@ def tile_moe_cas_glu_relu_kernel(tc, x_words, x_scales, w_words, w_scales, w1, w
         gate(5, bank[4])
         hidden_on_vector(h_low, 3, bank[7])
         results(0, 0, CHUNK, z_first[:], bank[5])
+        z_second = gates[3][:, :CHUNK]
+        second_product(bank[2][:, :CHUNK], 1, 0, CHUNK)
+        z_src = bank[2][:, :CHUNK]
         stage_up(5, bank[1])
         hidden_on_gpsimd(h_high, 5)
         light(1, 1, [bank[6], bank[5], bank[7]])
-        h_codes[CHUNK] = after_result.tile([P, 2 * CHUNK], U32, name="h_codes_pair", align_bytes=64, offset=0)
+        nc.vector.tensor_copy(z_second, z_src)
+        h_codes[CHUNK] = keep.tile([P, 2 * CHUNK], U32, name="h_codes_pair", align_bytes=64)
         quantize_hidden(h_pair[:], CHUNK, EARLY)
 
-        results(1, 0, CHUNK, ups[5][:, :CHUNK], bank[2])
+        nc.vector.tensor_copy(windows[1][:].indirect(offsets[:, : CHUNK // 16]), z_second)
         z_pair = keep.tile([P, 2 * CHUNK], F32, name="z_pair")
         gate(6, bank[6])
         results(0, CHUNK, EARLY, z_pair[:], bank[3])

@@ -20,6 +20,7 @@ ADD = mybir.AluOpType.add
 P = 128
 PACK = 4
 BANK = 512
+BANKS = 8
 GROUP = BANK // PACK
 GROUPS = S // GROUP
 CHUNK = 2 * GROUP
@@ -28,21 +29,20 @@ HALF = H // 2
 EARLY = S - CHUNK
 
 
-def load_scale_rows(nc, plane, scales):
+def load_scale_rows(nc, target, scales):
     rows = scales[0].rearrange("(q r) c -> r q c", r=4)
     for r in range(4):
-        nc.sync.dma_start(out=plane[r:P:32, :].bitcast(I32), in_=rows[r].bitcast(I32))
+        nc.sync.dma_start(out=target[r:P:32, :].bitcast(I32), in_=rows[r].bitcast(I32))
 
 
 def tile_moe_cas_glu_relu_kernel(tc, x_words, x_scales, w_words, w_scales, w1, w3, w2, offs, out):
     nc = tc.nc
     with ExitStack() as ctx:
         keep = ctx.enter_context(tc.tile_pool(name="keep", bufs=1))
-        after_gate = ctx.enter_context(tc.tile_pool(name="after_gate", bufs=1))
-        after_result = ctx.enter_context(tc.tile_pool(name="after_result", bufs=1))
+        after_w3 = ctx.enter_context(tc.tile_pool(name="after_w3", bufs=1))
         psum = ctx.enter_context(tc.psum_pool(name="psum", bufs=1))
 
-        bank = [psum.tile([P, BANK], F32, name=f"bank{i}") for i in range(8)]
+        bank = [psum.tile([P, BANK], F32, name=f"bank{i}") for i in range(BANKS)]
 
         offsets = keep.tile([P, S // 16], U16, name="offsets")
         x_plane = keep.tile([P, T], U8, name="x_plane", align_bytes=64)
@@ -53,7 +53,7 @@ def tile_moe_cas_glu_relu_kernel(tc, x_words, x_scales, w_words, w_scales, w1, w
         nc.vector.memset(w_plane[:].bitcast(I32), 0)
 
         raw = {(name, half): keep.tile([P, PACK, HALF], F32, name=f"{name}_raw{half}") for name, half in (("w1", 0), ("w1", 1), ("w3", 0))}
-        raw["w3", 1] = after_gate.tile([P, PACK, HALF], F32, name="w3_raw1", align_bytes=64, offset=0)
+        raw["w3", 1] = after_w3.tile([P, PACK, HALF], F32, name="w3_raw1", align_bytes=64, offset=0)
         w2_raw = keep.tile([P, PACK, N], F32, name="w2_raw")
 
         def load_half(name, w, half):
@@ -123,7 +123,7 @@ def tile_moe_cas_glu_relu_kernel(tc, x_words, x_scales, w_words, w_scales, w1, w
         w2_plane = keep.tile([P, N], U8, name="w2_plane", align_bytes=64)
         h_pair = grouped["w3"]
         w2_grouped = h_pair[:, : PACK * N]
-        slot_codes[EARLY] = after_gate.tile([P, S - EARLY], U32, name="late_codes", align_bytes=64, offset=0)
+        slot_codes[EARLY] = after_w3.tile([P, S - EARLY], U32, name="late_codes", align_bytes=64, offset=0)
         nc.vector.tensor_copy(slot_codes[EARLY][:], x_codes[:].bitcast(U32).indirect(offsets[:, EARLY // 16 :]))
         nc.gpsimd.tensor_scalar(w2_grouped.rearrange("p (c j) -> p c j", j=PACK), w2_raw[:].rearrange("p j c -> p c j"), 1.0, 0.0, MULT, ADD)
 
@@ -140,9 +140,10 @@ def tile_moe_cas_glu_relu_kernel(tc, x_words, x_scales, w_words, w_scales, w1, w
                 )
             return acc[:].rearrange("p (t s) -> p s t", t=PACK)
 
+        held_back, handed_on = 5, 2
         gates = {g: keep.tile([P, GROUP * PACK], F32, name=f"gate{g}") for g in range(GROUPS)}
-        ups = {g: keep.tile([P, GROUP * PACK], F32, name=f"up{g}") for g in range(ON_VECTOR, GROUPS) if g != 5}
-        ups[5] = gates[2]
+        ups = {g: keep.tile([P, GROUP * PACK], F32, name=f"up{g}") for g in range(ON_VECTOR, GROUPS) if g != held_back}
+        ups[held_back] = gates[handed_on]
 
         def by_slot(ap):
             return ap.rearrange("p (s t) -> p s t", t=PACK)
@@ -180,15 +181,15 @@ def tile_moe_cas_glu_relu_kernel(tc, x_words, x_scales, w_words, w_scales, w1, w
                 stop=True,
             )
 
-        def scatter(b, lo, z, acc):
-            nc.scalar.copy(out=z, in_=acc)
+        def scatter(b, lo, z):
             nc.vector.tensor_copy(windows[b][:].indirect(offsets[:, lo // 16 : (lo + z.shape[1]) // 16]), z)
 
-        def results(b, lo, hi, z, bank):
-            second_product(bank[:, : hi - lo], b, lo, hi)
-            scatter(b, lo, z, bank[:, : hi - lo])
+        def results(b, lo, hi, z, acc):
+            second_product(acc[:, : hi - lo], b, lo, hi)
+            nc.scalar.copy(out=z, in_=acc[:, : hi - lo])
+            scatter(b, lo, z)
 
-        z_first = after_result.tile([P, CHUNK], F32, name="z_first", align_bytes=64, offset=0)
+        z_first = keep.tile([P, CHUNK], F32, name="z_first")
         z_last = keep.tile([P, CHUNK], F32, name="z_last")
         z_end = keep.tile([P, 2 * CHUNK], F32, name="z_end")
         h_low, h_high = h_pair[:, : CHUNK * PACK], h_pair[:, CHUNK * PACK :]
@@ -199,6 +200,7 @@ def tile_moe_cas_glu_relu_kernel(tc, x_words, x_scales, w_words, w_scales, w1, w
         hidden_on_vector(h_high, 1, bank[7])
         nc.vector.quantize_mx(out=w2_codes[:].bitcast(FP8X4), scales=w2_plane[:], in_=w2_grouped)
         quantize_hidden(h_high, 0, CHUNK)
+
         gate(2, bank[2])
         gate(3, bank[3])
         gate(4, bank[5])
@@ -210,15 +212,14 @@ def tile_moe_cas_glu_relu_kernel(tc, x_words, x_scales, w_words, w_scales, w1, w
         results(0, 0, CHUNK, z_first[:], bank[5])
         z_second = gates[3][:, :CHUNK]
         second_product(bank[2][:, :CHUNK], 1, 0, CHUNK)
-        z_src = bank[2][:, :CHUNK]
         stage_up(5, bank[1])
         hidden_on_gpsimd(h_high, 5)
         light(1, 1, [bank[6], bank[5], bank[7]])
-        nc.vector.tensor_copy(z_second, z_src)
+        nc.vector.tensor_copy(z_second, bank[2][:, :CHUNK])
         h_codes[CHUNK] = keep.tile([P, 2 * CHUNK], U32, name="h_codes_pair", align_bytes=64)
         quantize_hidden(h_pair[:], CHUNK, EARLY)
 
-        nc.vector.tensor_copy(windows[1][:].indirect(offsets[:, : CHUNK // 16]), z_second)
+        scatter(1, 0, z_second)
         z_pair = keep.tile([P, 2 * CHUNK], F32, name="z_pair")
         gate(6, bank[6])
         results(0, CHUNK, EARLY, z_pair[:], bank[3])
@@ -235,6 +236,7 @@ def tile_moe_cas_glu_relu_kernel(tc, x_words, x_scales, w_words, w_scales, w1, w
         nc.sync.dma_start(out=out[0:P, :], in_=windows[0][:])
         second_product(bank[1][:, :CHUNK], 1, 2 * CHUNK, EARLY)
         second_product(bank[1][:, CHUNK:], 1, EARLY, S)
-        scatter(1, 2 * CHUNK, z_end[:], bank[1][:])
+        nc.scalar.copy(out=z_end[:], in_=bank[1][:])
+        scatter(1, 2 * CHUNK, z_end[:])
         nc.sync.dma_start(out=out[P : 2 * P, : T // 2], in_=windows[1][:, : T // 2])
         nc.scalar.dma_start(out=out[P : 2 * P, T // 2 :], in_=windows[1][:, T // 2 :])

@@ -14,6 +14,7 @@ U8 = mybir.dt.uint8
 FP8X4 = mybir.dt.float8_e4m3fn_x4
 FP4X4 = mybir.dt.float4_e2m1fn_x4
 RELU = mybir.ActivationFunctionType.Relu
+COPY = mybir.ActivationFunctionType.Copy
 MULT = mybir.AluOpType.mult
 ADD = mybir.AluOpType.add
 
@@ -24,7 +25,6 @@ BANKS = 8
 GROUP = BANK // PACK
 GROUPS = S // GROUP
 CHUNK = 2 * GROUP
-ON_VECTOR = GROUPS // 2
 HALF = H // 2
 EARLY = S - CHUNK
 
@@ -121,8 +121,7 @@ def tile_moe_cas_glu_relu_kernel(tc, x_words, x_scales, w_words, w_scales, w1, w
 
         w2_codes = keep.tile([P, N], U32, name="w2_codes", align_bytes=64)
         w2_plane = keep.tile([P, N], U8, name="w2_plane", align_bytes=64)
-        h_pair = grouped["w3"]
-        w2_grouped = h_pair[:, : PACK * N]
+        w2_grouped = grouped["w3"][:, : PACK * N]
         slot_codes[EARLY] = after_w3.tile([P, S - EARLY], U32, name="late_codes", align_bytes=64, offset=0)
         nc.vector.tensor_copy(slot_codes[EARLY][:], x_codes[:].bitcast(U32).indirect(offsets[:, EARLY // 16 :]))
         nc.gpsimd.tensor_scalar(w2_grouped.rearrange("p (c j) -> p c j", j=PACK), w2_raw[:].rearrange("p j c -> p c j"), 1.0, 0.0, MULT, ADD)
@@ -140,103 +139,61 @@ def tile_moe_cas_glu_relu_kernel(tc, x_words, x_scales, w_words, w_scales, w1, w
                 )
             return acc[:].rearrange("p (t s) -> p s t", t=PACK)
 
-        held_back, handed_on = 5, 2
-        gates = {g: keep.tile([P, GROUP * PACK], F32, name=f"gate{g}") for g in range(GROUPS)}
-        ups = {g: keep.tile([P, GROUP * PACK], F32, name=f"up{g}") for g in range(ON_VECTOR, GROUPS) if g != held_back}
-        ups[held_back] = gates[handed_on]
+        gates = [keep.tile([P, GROUP * PACK], F32, name=f"gate{g}") for g in range(GROUPS)]
+        h = [keep.tile([P, CHUNK * PACK], BF16, name=f"h{c}", align_bytes=64) for c in range(S // CHUNK)]
+        h_codes = keep.tile([P, S], U32, name="h_codes", align_bytes=64)
+        h_plane = keep.tile([P, S], U8, name="h_plane", align_bytes=64)
+        z = [keep.tile([P, S], F32, name=f"z{b}") for b in range(N // P)]
 
         def by_slot(ap):
             return ap.rearrange("p (s t) -> p s t", t=PACK)
 
-        def part(h, g):
-            lo = g % (CHUNK // GROUP) * GROUP * PACK
-            return h[:, lo : lo + GROUP * PACK]
-
         def gate(g, acc):
             nc.scalar.activation(out=by_slot(gates[g][:]), in_=first_product("w1", g, acc), func=RELU)
 
-        def hidden_on_vector(h, g, acc):
-            nc.vector.tensor_tensor(out=by_slot(part(h, g)), in0=first_product("w3", g, acc), in1=by_slot(gates[g][:]), op=MULT)
+        def hidden(g, acc):
+            lo = g % (CHUNK // GROUP) * GROUP * PACK
+            part = h[g * GROUP // CHUNK][:, lo : lo + GROUP * PACK]
+            nc.vector.tensor_tensor(out=by_slot(part), in0=first_product("w3", g, acc), in1=by_slot(gates[g][:]), op=MULT)
 
-        def stage_up(g, acc):
-            nc.scalar.copy(out=by_slot(ups[g][:]), in_=first_product("w3", g, acc))
+        def quantize_hidden(c):
+            cols = slice(c * CHUNK, (c + 1) * CHUNK)
+            nc.vector.quantize_mx(out=h_codes[:, cols].bitcast(FP8X4), scales=h_plane[:, cols], in_=h[c][:])
 
-        def hidden_on_gpsimd(h, g):
-            nc.gpsimd.tensor_tensor(out=part(h, g), in0=ups[g][:], in1=gates[g][:], op=MULT)
-
-        h_codes = {0: keep.tile([P, CHUNK], U32, name="h_codes_first", align_bytes=64)}
-        h_plane = keep.tile([P, S], U8, name="h_plane", align_bytes=64)
-
-        def quantize_hidden(h, lo, hi):
-            nc.vector.quantize_mx(out=words(h_codes, lo, hi), scales=h_plane[:, lo:hi], in_=h)
-
-        def second_product(acc, b, lo, hi):
+        def results(copy, b, lo, hi, acc):
             nc.tensor.matmul_mx(
-                out=acc,
+                out=acc[:, : hi - lo],
                 lhsT=w2_codes[:, b * P : (b + 1) * P].bitcast(FP8X4),
                 lhsT_scale=w2_plane[:, b * P : (b + 1) * P],
-                rhs=words(h_codes, lo, hi),
+                rhs=h_codes[:, lo:hi].bitcast(FP8X4),
                 rhs_scale=h_plane[:, lo:hi],
                 start=True,
                 stop=True,
             )
+            copy(out=z[b][:, lo:hi], in_=acc[:, : hi - lo])
 
-        def scatter(b, lo, z):
-            nc.vector.tensor_copy(windows[b][:].indirect(offsets[:, lo // 16 : (lo + z.shape[1]) // 16]), z)
+        def listed(b, lo, hi):
+            return windows[b][:].indirect(offsets[:, lo // 16 : hi // 16])
 
-        def results(b, lo, hi, z, acc):
-            second_product(acc[:, : hi - lo], b, lo, hi)
-            nc.scalar.copy(out=z, in_=acc[:, : hi - lo])
-            scatter(b, lo, z)
-
-        z_first = keep.tile([P, CHUNK], F32, name="z_first")
-        z_last = keep.tile([P, CHUNK], F32, name="z_last")
-        z_end = keep.tile([P, 2 * CHUNK], F32, name="z_end")
-        h_low, h_high = h_pair[:, : CHUNK * PACK], h_pair[:, CHUNK * PACK :]
-
-        gate(0, bank[0])
-        gate(1, bank[1])
-        hidden_on_vector(h_high, 0, bank[6])
-        hidden_on_vector(h_high, 1, bank[7])
-        nc.vector.quantize_mx(out=w2_codes[:].bitcast(FP8X4), scales=w2_plane[:], in_=w2_grouped)
-        quantize_hidden(h_high, 0, CHUNK)
-
-        gate(2, bank[2])
-        gate(3, bank[3])
-        gate(4, bank[5])
-        hidden_on_vector(h_low, 2, bank[6])
-        stage_up(4, bank[0])
-        hidden_on_gpsimd(h_high, 4)
-        gate(5, bank[4])
-        hidden_on_vector(h_low, 3, bank[7])
-        results(0, 0, CHUNK, z_first[:], bank[5])
-        z_second = gates[3][:, :CHUNK]
-        second_product(bank[2][:, :CHUNK], 1, 0, CHUNK)
-        stage_up(5, bank[1])
-        hidden_on_gpsimd(h_high, 5)
-        light(1, 1, [bank[6], bank[5], bank[7]])
-        nc.vector.tensor_copy(z_second, bank[2][:, :CHUNK])
-        h_codes[CHUNK] = keep.tile([P, 2 * CHUNK], U32, name="h_codes_pair", align_bytes=64)
-        quantize_hidden(h_pair[:], CHUNK, EARLY)
-
-        scatter(1, 0, z_second)
-        z_pair = keep.tile([P, 2 * CHUNK], F32, name="z_pair")
-        gate(6, bank[6])
-        results(0, CHUNK, EARLY, z_pair[:], bank[3])
-        stage_up(6, bank[5])
-        hidden_on_gpsimd(h_low, 6)
-        stage_up(7, bank[7])
-        gate(7, bank[3])
-        hidden_on_gpsimd(h_low, 7)
-        h_codes[EARLY] = keep.tile([P, CHUNK], U32, name="h_codes_last", align_bytes=64)
-        quantize_hidden(h_low, EARLY, S)
-        results(1, CHUNK, 2 * CHUNK, ups[7][:, :CHUNK], bank[4])
-
-        results(0, EARLY, S, z_last[:], bank[0])
+        ring = [bank[i] for i in (0, 1, 2, 3, 4)]
+        side = [bank[i] for i in (5, 6, 7)]
+        for g in range(GROUPS):
+            gate(g, ring[g % len(ring)])
+            hidden(g, side[g % len(side)])
+            if g == 1:
+                nc.vector.quantize_mx(out=w2_codes[:].bitcast(FP8X4), scales=w2_plane[:], in_=w2_grouped)
+            if g >= 2 and g % 2 == 0:
+                quantize_hidden(g // 2 - 1)
+        light(1, 1, [ring[3], ring[4], ring[0]])
+        results(nc.vector.tensor_copy, 1, 0, 2 * CHUNK, side[0])
+        quantize_hidden(3)
+        for c, acc in enumerate((ring[1], ring[2], ring[3], ring[4])):
+            lo, hi = c * CHUNK, (c + 1) * CHUNK
+            results(nc.scalar.copy, 0, lo, hi, acc)
+            nc.scalar.activation(out=listed(0, lo, hi), in_=z[0][:, lo:hi], func=COPY)
         nc.sync.dma_start(out=out[0:P, :], in_=windows[0][:])
-        second_product(bank[1][:, :CHUNK], 1, 2 * CHUNK, EARLY)
-        second_product(bank[1][:, CHUNK:], 1, EARLY, S)
-        nc.scalar.copy(out=z_end[:], in_=bank[1][:])
-        scatter(1, 2 * CHUNK, z_end[:])
+        nc.vector.tensor_copy(listed(1, 0, 2 * CHUNK), z[1][:, : 2 * CHUNK])
+        results(nc.vector.tensor_copy, 1, 2 * CHUNK, S, side[1])
+        nc.vector.tensor_copy(listed(1, 2 * CHUNK, S), z[1][:, 2 * CHUNK :])
         nc.sync.dma_start(out=out[P : 2 * P, : T // 2], in_=windows[1][:, : T // 2])
         nc.scalar.dma_start(out=out[P : 2 * P, T // 2 :], in_=windows[1][:, T // 2 :])

@@ -81,7 +81,7 @@ def tile_moe_cas_glu_relu_kernel(tc, x_words, x_scales, w_words, w_scales, w1, w
 
         windows = [keep.tile([P, T], F32, name=f"window{b}") for b in range(N // P)]
 
-        def light(b, first, y_banks):
+        def light(b, first, y_banks, copy=nc.scalar.copy):
             for c, y in enumerate(y_banks, first):
                 cols = slice(c * BANK, (c + 1) * BANK)
                 nc.tensor.matmul_mx(
@@ -93,7 +93,7 @@ def tile_moe_cas_glu_relu_kernel(tc, x_words, x_scales, w_words, w_scales, w1, w
                     start=True,
                     stop=True,
                 )
-                nc.scalar.copy(out=windows[b][:, cols], in_=y[:])
+                copy(out=windows[b][:, cols], in_=y[:])
 
         grouped = {name: keep.tile([P, PACK * H], BF16, name=f"{name}_grouped", align_bytes=64) for name in ("w1", "w3")}
         codes = {name: keep.tile([P, H], U32, name=f"{name}_codes", align_bytes=64) for name in ("w1", "w3")}
@@ -184,7 +184,8 @@ def tile_moe_cas_glu_relu_kernel(tc, x_words, x_scales, w_words, w_scales, w1, w
                 nc.vector.quantize_mx(out=w2_codes[:].bitcast(FP8X4), scales=w2_plane[:], in_=w2_grouped)
             if g >= 2 and g % 2 == 0:
                 quantize_hidden(g // 2 - 1)
-        light(1, 1, [ring[3], ring[4], ring[0]])
+        light(1, 1, [ring[3], ring[4]])
+        light(1, 3, [side[2]], nc.vector.tensor_copy)
         results(nc.vector.tensor_copy, 1, 0, 2 * CHUNK, side[0])
         quantize_hidden(3)
         for c, acc in enumerate((ring[1], ring[2], ring[3], ring[4])):

@@ -52,8 +52,8 @@ def tile_moe_cas_glu_relu_kernel(tc, x_words, x_scales, w_words, w_scales, w1, w
         nc.vector.memset(x_plane[:].bitcast(I32), 0)
         nc.vector.memset(w_plane[:].bitcast(I32), 0)
 
-        raw = {(name, half): keep.tile([P, PACK, HALF], F32, name=f"{name}_raw{half}") for name, half in (("w1", 0), ("w1", 1), ("w3", 0))}
-        raw["w3", 1] = after_w3.tile([P, PACK, HALF], F32, name="w3_raw1", align_bytes=64, offset=0)
+        raw = {(name, half): keep.tile([P, PACK, HALF], F32, name=f"{name}_raw{half}") for name, half in (("w1", 0), ("w1", 1))}
+        w3_raw = after_w3.tile([P, PACK, H], F32, name="w3_raw", align_bytes=64, offset=0)
         w2_raw = keep.tile([P, PACK, N], F32, name="w2_raw")
 
         def load_half(name, w, half):
@@ -66,8 +66,7 @@ def tile_moe_cas_glu_relu_kernel(tc, x_words, x_scales, w_words, w_scales, w1, w
         nc.sync.dma_start(out=w_codes[:].bitcast(I32), in_=w_words[0].bitcast(I32))
         load_scale_rows(nc, w_plane, w_scales)
         load_half("w1", w1, 1)
-        load_half("w3", w3, 0)
-        load_half("w3", w3, 1)
+        nc.sync.dma_start(out=w3_raw[:], in_=w3.rearrange("(p j) c -> p j c", j=PACK))
         nc.sync.dma_start(out=w2_raw[:], in_=w2.rearrange("(p j) c -> p j c", j=PACK))
 
         slot_plane = keep.tile([P, S], U8, name="slot_plane", align_bytes=64)
@@ -81,11 +80,12 @@ def tile_moe_cas_glu_relu_kernel(tc, x_words, x_scales, w_words, w_scales, w1, w
 
         windows = [keep.tile([P, T], F32, name=f"window{b}") for b in range(N // P)]
 
-        def light(b, first, y_banks, copy=nc.scalar.copy):
-            for c, y in enumerate(y_banks, first):
-                cols = slice(c * BANK, (c + 1) * BANK)
+        def light(b, first, y_banks, copy=nc.scalar.copy, width=BANK):
+            for c, acc in enumerate(y_banks, first):
+                cols = slice(c * width, (c + 1) * width)
+                y = acc[:, :width]
                 nc.tensor.matmul_mx(
-                    out=y[:],
+                    out=y,
                     lhsT=w_codes[:, 2 * P * b : 2 * P * (b + 1)].bitcast(FP4X4),
                     lhsT_scale=w_plane[:, P * b : P * (b + 1)],
                     rhs=x_codes[:, cols].bitcast(FP8X4),
@@ -93,7 +93,7 @@ def tile_moe_cas_glu_relu_kernel(tc, x_words, x_scales, w_words, w_scales, w1, w
                     start=True,
                     stop=True,
                 )
-                copy(out=windows[b][:, cols], in_=y[:])
+                copy(out=windows[b][:, cols], in_=y)
 
         grouped = {name: keep.tile([P, PACK * H], BF16, name=f"{name}_grouped", align_bytes=64) for name in ("w1", "w3")}
         codes = {name: keep.tile([P, H], U32, name=f"{name}_codes", align_bytes=64) for name in ("w1", "w3")}
@@ -113,8 +113,7 @@ def tile_moe_cas_glu_relu_kernel(tc, x_words, x_scales, w_words, w_scales, w1, w
         regroup(nc.scalar.copy, "w1", 0)
         regroup(nc.vector.tensor_copy, "w1", 1)
         quantize_first("w1", 1)
-        regroup(nc.vector.tensor_copy, "w3", 0)
-        regroup(nc.vector.tensor_copy, "w3", 1)
+        nc.vector.tensor_copy(out=grouped["w3"][:].rearrange("p (t m j) -> p m j t", t=PACK, j=PACK), in_=w3_raw[:].rearrange("p j (m t) -> p m j t", t=PACK))
         quantize_first("w3", PACK)
         light(0, 0, bank[:4])
         light(1, 0, bank[4:5])
@@ -185,7 +184,8 @@ def tile_moe_cas_glu_relu_kernel(tc, x_words, x_scales, w_words, w_scales, w1, w
             if g >= 2 and g % 2 == 0:
                 quantize_hidden(g // 2 - 1)
         light(1, 1, [ring[3], ring[4]])
-        light(1, 3, [side[2]], nc.vector.tensor_copy)
+        light(1, 6, [ring[0]], width=CHUNK)
+        light(1, 7, [side[2]], nc.vector.tensor_copy, CHUNK)
         results(nc.vector.tensor_copy, 1, 0, 2 * CHUNK, side[0])
         quantize_hidden(3)
         for c, acc in enumerate((ring[1], ring[2], ring[3], ring[4])):

@@ -114,7 +114,7 @@ def tile_moe_cas_glu_relu_kernel(tc, x_words, x_scales, w_words, w_scales, w1, w
         regroup(nc.vector.tensor_copy, "w1", 1)
         quantize_first("w1", 1)
         nc.vector.tensor_copy(out=grouped["w3"][:].rearrange("p (t m j) -> p m j t", t=PACK, j=PACK), in_=w3_raw[:].rearrange("p j (m t) -> p m j t", t=PACK))
-        quantize_first("w3", PACK)
+        quantize_first("w3", 2)
         light(0, 0, bank[:4])
         light(1, 0, bank[4:5])
 
@@ -159,17 +159,20 @@ def tile_moe_cas_glu_relu_kernel(tc, x_words, x_scales, w_words, w_scales, w1, w
             cols = slice(c * CHUNK, (c + 1) * CHUNK)
             nc.vector.quantize_mx(out=h_codes[:, cols].bitcast(FP8X4), scales=h_plane[:, cols], in_=h[c][:])
 
-        def results(copy, b, lo, hi, acc):
-            nc.tensor.matmul_mx(
-                out=acc[:, : hi - lo],
-                lhsT=w2_codes[:, b * P : (b + 1) * P].bitcast(FP8X4),
-                lhsT_scale=w2_plane[:, b * P : (b + 1) * P],
-                rhs=h_codes[:, lo:hi].bitcast(FP8X4),
-                rhs_scale=h_plane[:, lo:hi],
-                start=True,
-                stop=True,
-            )
-            copy(out=z[b][:, lo:hi], in_=acc[:, : hi - lo])
+        def results(c, acc):
+            lo, hi = c * CHUNK, (c + 1) * CHUNK
+            for b in range(N // P):
+                nc.tensor.matmul_mx(
+                    out=acc[:, b * CHUNK : (b + 1) * CHUNK],
+                    lhsT=w2_codes[:, b * P : (b + 1) * P].bitcast(FP8X4),
+                    lhsT_scale=w2_plane[:, b * P : (b + 1) * P],
+                    rhs=h_codes[:, lo:hi].bitcast(FP8X4),
+                    rhs_scale=h_plane[:, lo:hi],
+                    start=True,
+                    stop=True,
+                )
+            for b in range(N // P):
+                nc.scalar.copy(out=z[b][:, lo:hi], in_=acc[:, b * CHUNK : (b + 1) * CHUNK])
 
         def listed(b, lo, hi):
             return windows[b][:].indirect(offsets[:, lo // 16 : hi // 16])
@@ -183,18 +186,14 @@ def tile_moe_cas_glu_relu_kernel(tc, x_words, x_scales, w_words, w_scales, w1, w
                 nc.vector.quantize_mx(out=w2_codes[:].bitcast(FP8X4), scales=w2_plane[:], in_=w2_grouped)
             if g >= 2 and g % 2 == 0:
                 quantize_hidden(g // 2 - 1)
-        light(1, 1, [ring[3], ring[4]])
-        light(1, 6, [ring[0]], width=CHUNK)
-        light(1, 7, [side[2]], nc.vector.tensor_copy, CHUNK)
-        results(nc.vector.tensor_copy, 1, 0, 2 * CHUNK, side[0])
+        light(1, 1, [ring[3]])
+        light(1, 2, [side[2], side[0]], nc.vector.tensor_copy)
         quantize_hidden(3)
-        for c, acc in enumerate((ring[1], ring[2], ring[3], ring[4])):
+        for c, acc in enumerate((ring[1], ring[2], ring[4], ring[0])):
             lo, hi = c * CHUNK, (c + 1) * CHUNK
-            results(nc.scalar.copy, 0, lo, hi, acc)
+            results(c, acc)
             nc.scalar.activation(out=listed(0, lo, hi), in_=z[0][:, lo:hi], func=COPY)
-        nc.sync.dma_start(out=out[0:P, :], in_=windows[0][:])
-        nc.vector.tensor_copy(listed(1, 0, 2 * CHUNK), z[1][:, : 2 * CHUNK])
-        results(nc.vector.tensor_copy, 1, 2 * CHUNK, S, side[1])
-        nc.vector.tensor_copy(listed(1, 2 * CHUNK, S), z[1][:, 2 * CHUNK :])
-        nc.sync.dma_start(out=out[P : 2 * P, : T // 2], in_=windows[1][:, : T // 2])
-        nc.scalar.dma_start(out=out[P : 2 * P, T // 2 :], in_=windows[1][:, T // 2 :])
+        nc.scalar.dma_start(out=out[0:P, :], in_=windows[0][:])
+        for lo, hi in ((0, 2 * CHUNK), (2 * CHUNK, S)):
+            nc.vector.tensor_copy(listed(1, lo, hi), z[1][:, lo:hi])
+        nc.sync.dma_start(out=out[P : 2 * P, :], in_=windows[1][:])

@@ -25,8 +25,12 @@ BANKS = 8
 GROUP = BANK // PACK
 GROUPS = S // GROUP
 CHUNK = 2 * GROUP
+CHUNKS = S // CHUNK
 HALF = H // 2
-EARLY = S - CHUNK
+BLOCK_ROWS = 8
+HALF_BLOCKS = HALF // (BLOCK_ROWS * PACK)
+RING = 5
+EARLY = RING * GROUP
 
 
 def load_scale_rows(nc, target, scales):
@@ -52,8 +56,8 @@ def tile_moe_cas_glu_relu_kernel(tc, x_words, x_scales, w_words, w_scales, w1, w
         nc.vector.memset(x_plane[:].bitcast(I32), 0)
         nc.vector.memset(w_plane[:].bitcast(I32), 0)
 
-        raw = {(name, half): keep.tile([P, PACK, HALF], F32, name=f"{name}_raw{half}") for name, half in (("w1", 0), ("w1", 1))}
-        w3_raw = after_w3.tile([P, PACK, H], F32, name="w3_raw", align_bytes=64, offset=0)
+        raw = {(name, half): keep.tile([P, PACK, HALF], F32, name=f"{name}_raw{half}") for name, half in (("w1", 0), ("w1", 1), ("w3", 0))}
+        raw["w3", 1] = after_w3.tile([P, PACK, HALF], F32, name="w3_raw1", align_bytes=64, offset=0)
         w2_raw = keep.tile([P, PACK, N], F32, name="w2_raw")
 
         def load_half(name, w, half):
@@ -66,26 +70,28 @@ def tile_moe_cas_glu_relu_kernel(tc, x_words, x_scales, w_words, w_scales, w1, w
         nc.sync.dma_start(out=w_codes[:].bitcast(I32), in_=w_words[0].bitcast(I32))
         load_scale_rows(nc, w_plane, w_scales)
         load_half("w1", w1, 1)
-        nc.sync.dma_start(out=w3_raw[:], in_=w3.rearrange("(p j) c -> p j c", j=PACK))
-        nc.sync.dma_start(out=w2_raw[:], in_=w2.rearrange("(p j) c -> p j c", j=PACK))
+        load_half("w3", w3, 0)
+        load_half("w3", w3, 1)
+        w2_rows = w2.rearrange("(q u r e) c -> u q r (e c)", u=2, r=BLOCK_ROWS, e=2)
+        for u in range(2):
+            nc.sync.dma_start(out=w2_raw[:, 2 * u : 2 * u + 2, :].rearrange("p e c -> p (e c)"), in_=w2_rows[u])
 
         slot_plane = keep.tile([P, S], U8, name="slot_plane", align_bytes=64)
         slot_codes = {0: keep.tile([P, EARLY], U32, name="early_codes", align_bytes=64)}
         nc.vector.tensor_copy(slot_plane[:], x_plane[:].indirect(offsets[:]))
         nc.vector.tensor_copy(slot_codes[0][:], x_codes[:].bitcast(U32).indirect(offsets[:, : EARLY // 16]))
 
-        def words(tiles, lo, hi):
-            first = max(k for k in tiles if k <= lo)
-            return tiles[first][:, lo - first : hi - first].bitcast(FP8X4)
+        def words(lo, hi):
+            first = max(start for start in slot_codes if start <= lo)
+            return slot_codes[first][:, lo - first : hi - first].bitcast(FP8X4)
 
         windows = [keep.tile([P, T], F32, name=f"window{b}") for b in range(N // P)]
 
-        def light(b, first, y_banks, copy=nc.scalar.copy, width=BANK):
-            for c, acc in enumerate(y_banks, first):
-                cols = slice(c * width, (c + 1) * width)
-                y = acc[:, :width]
+        def light(b, first, y_banks, copy):
+            for n, acc in enumerate(y_banks, first):
+                cols = slice(n * BANK, (n + 1) * BANK)
                 nc.tensor.matmul_mx(
-                    out=y,
+                    out=acc[:],
                     lhsT=w_codes[:, 2 * P * b : 2 * P * (b + 1)].bitcast(FP4X4),
                     lhsT_scale=w_plane[:, P * b : P * (b + 1)],
                     rhs=x_codes[:, cols].bitcast(FP8X4),
@@ -93,30 +99,33 @@ def tile_moe_cas_glu_relu_kernel(tc, x_words, x_scales, w_words, w_scales, w1, w
                     start=True,
                     stop=True,
                 )
-                copy(out=windows[b][:, cols], in_=y)
+                copy(out=windows[b][:, cols], in_=acc[:])
 
         grouped = {name: keep.tile([P, PACK * H], BF16, name=f"{name}_grouped", align_bytes=64) for name in ("w1", "w3")}
         codes = {name: keep.tile([P, H], U32, name=f"{name}_codes", align_bytes=64) for name in ("w1", "w3")}
         plane = {name: keep.tile([P, H], U8, name=f"{name}_plane", align_bytes=64) for name in ("w1", "w3")}
 
         def regroup(copy, name, half):
-            m = slice(half * P // 2, (half + 1) * P // 2)
-            whole = grouped[name][:].rearrange("p (t m j) -> p t m j", t=PACK, j=PACK)
-            copy(out=whole[:, :, m, :].rearrange("p t m j -> p m j t"), in_=raw[name, half][:].rearrange("p j (m t) -> p m j t", t=PACK))
+            blocks = slice(half * HALF_BLOCKS, (half + 1) * HALF_BLOCKS)
+            target = grouped[name][:].rearrange("p (u e q r j) -> p u q r j e", u=2, e=2, r=BLOCK_ROWS, j=PACK)
+            source = raw[name, half][:].rearrange("p j (q u r e) -> p u q r j e", u=2, r=BLOCK_ROWS, e=2)
+            for u in (1, 0):
+                copy(out=target[:, u, blocks], in_=source[:, u])
 
-        def quantize_first(name, pieces):
-            step = H // pieces
-            for lo in reversed(range(0, H, step)):
-                cols = slice(lo, lo + step)
-                nc.vector.quantize_mx(out=codes[name][:, cols].bitcast(FP8X4), scales=plane[name][:, cols], in_=grouped[name][:, PACK * lo : PACK * (lo + step)])
+        def quantize_first(name):
+            for u in (1, 0):
+                lo, hi = u * 2 * P, (u + 1) * 2 * P
+                nc.vector.quantize_mx(out=codes[name][:, lo:hi].bitcast(FP8X4), scales=plane[name][:, lo:hi], in_=grouped[name][:, PACK * lo : PACK * hi])
 
         regroup(nc.scalar.copy, "w1", 0)
         regroup(nc.vector.tensor_copy, "w1", 1)
-        quantize_first("w1", 1)
-        nc.vector.tensor_copy(out=grouped["w3"][:].rearrange("p (t m j) -> p m j t", t=PACK, j=PACK), in_=w3_raw[:].rearrange("p j (m t) -> p m j t", t=PACK))
-        quantize_first("w3", 2)
-        light(0, 0, bank[:4])
-        light(1, 0, bank[4:5])
+        quantize_first("w1")
+        regroup(nc.vector.tensor_copy, "w3", 0)
+        regroup(nc.vector.tensor_copy, "w3", 1)
+        quantize_first("w3")
+        ring, side = bank[:RING], bank[RING:]
+        light(0, 0, ring[: T // BANK], nc.scalar.copy)
+        light(1, 0, ring[T // BANK :], nc.scalar.copy)
 
         w2_codes = keep.tile([P, N], U32, name="w2_codes", align_bytes=64)
         w2_plane = keep.tile([P, N], U8, name="w2_plane", align_bytes=64)
@@ -131,7 +140,7 @@ def tile_moe_cas_glu_relu_kernel(tc, x_words, x_scales, w_words, w_scales, w1, w
                     out=acc[:, t * GROUP : (t + 1) * GROUP],
                     lhsT=codes[name][:, t * P : (t + 1) * P].bitcast(FP8X4),
                     lhsT_scale=plane[name][:, t * P : (t + 1) * P],
-                    rhs=words(slot_codes, g * GROUP, (g + 1) * GROUP),
+                    rhs=words(g * GROUP, (g + 1) * GROUP),
                     rhs_scale=slot_plane[:, g * GROUP : (g + 1) * GROUP],
                     start=True,
                     stop=True,
@@ -139,7 +148,7 @@ def tile_moe_cas_glu_relu_kernel(tc, x_words, x_scales, w_words, w_scales, w1, w
             return acc[:].rearrange("p (t s) -> p s t", t=PACK)
 
         gates = [keep.tile([P, GROUP * PACK], F32, name=f"gate{g}") for g in range(GROUPS)]
-        h = [keep.tile([P, CHUNK * PACK], BF16, name=f"h{c}", align_bytes=64) for c in range(S // CHUNK)]
+        h = [keep.tile([P, CHUNK * PACK], BF16, name=f"h{c}", align_bytes=64) for c in range(CHUNKS)]
         h_codes = keep.tile([P, S], U32, name="h_codes", align_bytes=64)
         h_plane = keep.tile([P, S], U8, name="h_plane", align_bytes=64)
         z = [keep.tile([P, S], F32, name=f"z{b}") for b in range(N // P)]
@@ -177,8 +186,6 @@ def tile_moe_cas_glu_relu_kernel(tc, x_words, x_scales, w_words, w_scales, w1, w
         def listed(b, lo, hi):
             return windows[b][:].indirect(offsets[:, lo // 16 : hi // 16])
 
-        ring = [bank[i] for i in (0, 1, 2, 3, 4)]
-        side = [bank[i] for i in (5, 6, 7)]
         for g in range(GROUPS):
             gate(g, ring[g % len(ring)])
             hidden(g, side[g % len(side)])
@@ -186,14 +193,17 @@ def tile_moe_cas_glu_relu_kernel(tc, x_words, x_scales, w_words, w_scales, w1, w
                 nc.vector.quantize_mx(out=w2_codes[:].bitcast(FP8X4), scales=w2_plane[:], in_=w2_grouped)
             if g >= 2 and g % 2 == 0:
                 quantize_hidden(g // 2 - 1)
-        light(1, 1, [ring[3]])
-        light(1, 2, [side[2], side[0]], nc.vector.tensor_copy)
-        quantize_hidden(3)
-        for c, acc in enumerate((ring[1], ring[2], ring[4], ring[0])):
+
+        light(1, 1, [ring[3]], nc.scalar.copy)
+        light(1, 2, [side[5 % len(side)], side[6 % len(side)]], nc.vector.tensor_copy)
+        quantize_hidden(CHUNKS - 1)
+
+        for c, g in enumerate((6, 7, 4, 5)):
             lo, hi = c * CHUNK, (c + 1) * CHUNK
-            results(c, acc)
+            results(c, ring[g % len(ring)])
             nc.scalar.activation(out=listed(0, lo, hi), in_=z[0][:, lo:hi], func=COPY)
         nc.scalar.dma_start(out=out[0:P, :], in_=windows[0][:])
-        for lo, hi in ((0, 2 * CHUNK), (2 * CHUNK, S)):
-            nc.vector.tensor_copy(listed(1, lo, hi), z[1][:, lo:hi])
+
+        for lo in (0, S // 2):
+            nc.vector.tensor_copy(listed(1, lo, lo + S // 2), z[1][:, lo : lo + S // 2])
         nc.sync.dma_start(out=out[P : 2 * P, :], in_=windows[1][:])

@@ -27,8 +27,6 @@ GROUPS = S // GROUP
 CHUNK = 2 * GROUP
 CHUNKS = S // CHUNK
 HALF = H // 2
-BLOCK_ROWS = 8
-HALF_BLOCKS = HALF // (BLOCK_ROWS * PACK)
 RING = 5
 EARLY = RING * GROUP
 
@@ -72,9 +70,7 @@ def tile_moe_cas_glu_relu_kernel(tc, x_words, x_scales, w_words, w_scales, w1, w
         load_half("w1", w1, 1)
         load_half("w3", w3, 0)
         load_half("w3", w3, 1)
-        w2_rows = w2.rearrange("(q u r e) c -> u q r (e c)", u=2, r=BLOCK_ROWS, e=2)
-        for u in range(2):
-            nc.sync.dma_start(out=w2_raw[:, 2 * u : 2 * u + 2, :].rearrange("p e c -> p (e c)"), in_=w2_rows[u])
+        nc.sync.dma_start(out=w2_raw[:], in_=w2.rearrange("(p j) c -> p j c", j=PACK))
 
         slot_plane = keep.tile([P, S], U8, name="slot_plane", align_bytes=64)
         slot_codes = {0: keep.tile([P, EARLY], U32, name="early_codes", align_bytes=64)}
@@ -106,23 +102,22 @@ def tile_moe_cas_glu_relu_kernel(tc, x_words, x_scales, w_words, w_scales, w1, w
         plane = {name: keep.tile([P, H], U8, name=f"{name}_plane", align_bytes=64) for name in ("w1", "w3")}
 
         def regroup(copy, name, half):
-            blocks = slice(half * HALF_BLOCKS, (half + 1) * HALF_BLOCKS)
-            target = grouped[name][:].rearrange("p (u e q r j) -> p u q r j e", u=2, e=2, r=BLOCK_ROWS, j=PACK)
-            source = raw[name, half][:].rearrange("p j (q u r e) -> p u q r j e", u=2, r=BLOCK_ROWS, e=2)
-            for u in (1, 0):
-                copy(out=target[:, u, blocks], in_=source[:, u])
+            m = slice(half * P // 2, (half + 1) * P // 2)
+            whole = grouped[name][:].rearrange("p (t m j) -> p t m j", t=PACK, j=PACK)
+            copy(out=whole[:, :, m, :].rearrange("p t m j -> p m j t"), in_=raw[name, half][:].rearrange("p j (m t) -> p m j t", t=PACK))
 
-        def quantize_first(name):
-            for u in (1, 0):
-                lo, hi = u * 2 * P, (u + 1) * 2 * P
-                nc.vector.quantize_mx(out=codes[name][:, lo:hi].bitcast(FP8X4), scales=plane[name][:, lo:hi], in_=grouped[name][:, PACK * lo : PACK * hi])
+        def quantize_first(name, pieces):
+            step = H // pieces
+            for lo in reversed(range(0, H, step)):
+                cols = slice(lo, lo + step)
+                nc.vector.quantize_mx(out=codes[name][:, cols].bitcast(FP8X4), scales=plane[name][:, cols], in_=grouped[name][:, PACK * lo : PACK * (lo + step)])
 
         regroup(nc.scalar.copy, "w1", 0)
         regroup(nc.vector.tensor_copy, "w1", 1)
-        quantize_first("w1")
+        quantize_first("w1", 1)
         regroup(nc.vector.tensor_copy, "w3", 0)
         regroup(nc.vector.tensor_copy, "w3", 1)
-        quantize_first("w3")
+        quantize_first("w3", 2)
         ring, side = bank[:RING], bank[RING:]
         light(0, 0, ring[: T // BANK], nc.scalar.copy)
         light(1, 0, ring[T // BANK :], nc.scalar.copy)

@@ -26,15 +26,9 @@ GROUP = BANK // PACK
 GROUPS = S // GROUP
 CHUNK = 2 * GROUP
 CHUNKS = S // CHUNK
+W1_CUTS = (0, 192, 352, 512)
 HALF = H // 2
-RING = 5
-EARLY = RING * GROUP
-
-
-def load_scale_rows(nc, target, scales):
-    rows = scales[0].rearrange("(q r) c -> r q c", r=4)
-    for r in range(4):
-        nc.sync.dma_start(out=target[r:P:32, :].bitcast(I32), in_=rows[r].bitcast(I32))
+SPLIT = 1280
 
 
 def tile_moe_cas_glu_relu_kernel(tc, x_words, x_scales, w_words, w_scales, w1, w3, w2, offs, out):
@@ -54,57 +48,71 @@ def tile_moe_cas_glu_relu_kernel(tc, x_words, x_scales, w_words, w_scales, w1, w
         nc.vector.memset(x_plane[:].bitcast(I32), 0)
         nc.vector.memset(w_plane[:].bitcast(I32), 0)
 
-        raw = {(name, half): keep.tile([P, PACK, HALF], F32, name=f"{name}_raw{half}") for name, half in (("w1", 0), ("w1", 1), ("w3", 0))}
-        raw["w3", 1] = after_w3.tile([P, PACK, HALF], F32, name="w3_raw1", align_bytes=64, offset=0)
+        def load_scale_row(queue, target, scales, r):
+            rows = scales[0].rearrange("(q r) c -> r q c", r=4)
+            queue.dma_start(out=target[r:P:32, :].bitcast(I32), in_=rows[r].bitcast(I32))
+
+        def load_columns(queue, raw, w, lo, hi):
+            queue.dma_start(out=raw[:], in_=w[:, lo:hi].rearrange("(p j) c -> p j c", j=PACK))
+
+        w1_cols = list(zip(W1_CUTS, W1_CUTS[1:]))
+        w1_raw = [keep.tile([P, PACK, hi - lo], F32, name=f"w1_raw{lo}") for lo, hi in w1_cols]
+        w3_raw = [keep.tile([P, PACK, HALF], F32, name="w3_raw0"), after_w3.tile([P, PACK, HALF], F32, name="w3_raw1", offset=0)]
         w2_raw = keep.tile([P, PACK, N], F32, name="w2_raw")
-
-        def load_half(name, w, half):
-            nc.sync.dma_start(out=raw[name, half][:], in_=w[:, half * HALF : (half + 1) * HALF].rearrange("(p j) c -> p j c", j=PACK))
-
-        load_half("w1", w1, 0)
-        load_scale_rows(nc, x_plane, x_scales)
-        nc.sync.dma_start(offsets[:], offs)
-        nc.sync.dma_start(out=x_codes[:], in_=x_words[0].rearrange("p t d -> p (t d)").bitcast(I32))
-        nc.sync.dma_start(out=w_codes[:].bitcast(I32), in_=w_words[0].bitcast(I32))
-        load_scale_rows(nc, w_plane, w_scales)
-        load_half("w1", w1, 1)
-        load_half("w3", w3, 0)
-        load_half("w3", w3, 1)
-        nc.sync.dma_start(out=w2_raw[:], in_=w2.rearrange("(p j) c -> p j c", j=PACK))
-
-        slot_plane = keep.tile([P, S], U8, name="slot_plane", align_bytes=64)
-        slot_codes = {0: keep.tile([P, EARLY], U32, name="early_codes", align_bytes=64)}
-        nc.vector.tensor_copy(slot_plane[:], x_plane[:].indirect(offsets[:]))
-        nc.vector.tensor_copy(slot_codes[0][:], x_codes[:].bitcast(U32).indirect(offsets[:, : EARLY // 16]))
-
-        def words(lo, hi):
-            first = max(start for start in slot_codes if start <= lo)
-            return slot_codes[first][:, lo - first : hi - first].bitcast(FP8X4)
-
-        windows = [keep.tile([P, T], F32, name=f"window{b}") for b in range(N // P)]
-
-        def light(b, first, y_banks, copy):
-            for n, acc in enumerate(y_banks, first):
-                cols = slice(n * BANK, (n + 1) * BANK)
-                nc.tensor.matmul_mx(
-                    out=acc[:],
-                    lhsT=w_codes[:, 2 * P * b : 2 * P * (b + 1)].bitcast(FP4X4),
-                    lhsT_scale=w_plane[:, P * b : P * (b + 1)],
-                    rhs=x_codes[:, cols].bitcast(FP8X4),
-                    rhs_scale=x_plane[:, cols],
-                    start=True,
-                    stop=True,
-                )
-                copy(out=windows[b][:, cols], in_=acc[:])
 
         grouped = {name: keep.tile([P, PACK * H], BF16, name=f"{name}_grouped", align_bytes=64) for name in ("w1", "w3")}
         codes = {name: keep.tile([P, H], U32, name=f"{name}_codes", align_bytes=64) for name in ("w1", "w3")}
         plane = {name: keep.tile([P, H], U8, name=f"{name}_plane", align_bytes=64) for name in ("w1", "w3")}
 
-        def regroup(copy, name, half):
-            m = slice(half * P // 2, (half + 1) * P // 2)
+        def regrouped(name, raw, lo, hi, walk):
             whole = grouped[name][:].rearrange("p (t m j) -> p t m j", t=PACK, j=PACK)
-            copy(out=whole[:, :, m, :].rearrange("p t m j -> p m j t"), in_=raw[name, half][:].rearrange("p j (m t) -> p m j t", t=PACK))
+            return (
+                whole[:, :, lo // PACK : hi // PACK, :].rearrange("p t m j -> p " + walk),
+                raw[:].rearrange("p j (m t) -> p " + walk, t=PACK),
+            )
+
+        def round_columns(copy, name, raw, lo, hi):
+            target, source = regrouped(name, raw, lo, hi, "m j t")
+            copy(out=target, in_=source)
+
+        load_columns(nc.sync, w1_raw[0], w1, *w1_cols[0])
+        nc.sync.dma_start(offsets[:], offs)
+        nc.sync.dma_start(out=w_codes[:].bitcast(I32), in_=w_words[0].bitcast(I32))
+        for r in range(4):
+            load_scale_row(nc.sync, x_plane, x_scales, r)
+        nc.sync.dma_start(out=x_codes[:], in_=x_words[0].rearrange("p t d -> p (t d)").bitcast(I32))
+        for r in range(4):
+            load_scale_row(nc.sync, w_plane, w_scales, r)
+        for i in (1, 2):
+            load_columns(nc.sync, w1_raw[i], w1, *w1_cols[i])
+        for i in range(2):
+            load_columns(nc.sync, w3_raw[i], w3, i * HALF, (i + 1) * HALF)
+        nc.sync.dma_start(out=w2_raw[:], in_=w2.rearrange("(p j) c -> p j c", j=PACK))
+
+        slot_plane = keep.tile([P, S], U8, name="slot_plane", align_bytes=64)
+        slot_codes = keep.tile([P, S], U32, name="slot_codes", align_bytes=64)
+        nc.vector.tensor_copy(slot_plane[:], x_plane[:].indirect(offsets[:]))
+        nc.vector.tensor_copy(slot_codes[:], x_codes[:].bitcast(U32).indirect(offsets[:]))
+
+        round_columns(nc.scalar.copy, "w1", w1_raw[0], *w1_cols[0])
+        for i in (1, 2):
+            target, source = regrouped("w1", w1_raw[i], *w1_cols[i], "m t j")
+            nc.gpsimd.tensor_scalar(target, source, 1.0, 0.0, MULT, ADD)
+
+        windows = [keep.tile([P, T], F32, name=f"window{b}") for b in range(N // P)]
+
+        def light(b, lo, hi, acc, copy):
+            cols = slice(lo, hi)
+            nc.tensor.matmul_mx(
+                out=acc[:, : hi - lo],
+                lhsT=w_codes[:, 2 * P * b : 2 * P * (b + 1)].bitcast(FP4X4),
+                lhsT_scale=w_plane[:, P * b : P * (b + 1)],
+                rhs=x_codes[:, cols].bitcast(FP8X4),
+                rhs_scale=x_plane[:, cols],
+                start=True,
+                stop=True,
+            )
+            copy(out=windows[b][:, cols], in_=acc[:, : hi - lo])
 
         def quantize_first(name, pieces):
             step = H // pieces
@@ -112,21 +120,18 @@ def tile_moe_cas_glu_relu_kernel(tc, x_words, x_scales, w_words, w_scales, w1, w
                 cols = slice(lo, lo + step)
                 nc.vector.quantize_mx(out=codes[name][:, cols].bitcast(FP8X4), scales=plane[name][:, cols], in_=grouped[name][:, PACK * lo : PACK * (lo + step)])
 
-        regroup(nc.scalar.copy, "w1", 0)
-        regroup(nc.vector.tensor_copy, "w1", 1)
+        early = [(b, lo, min(lo + BANK, stop)) for b, stop in ((0, T), (1, SPLIT)) for lo in range(0, stop, BANK)]
+        for acc, part in zip(bank, early):
+            light(*part, acc, nc.scalar.copy)
+
         quantize_first("w1", 1)
-        regroup(nc.vector.tensor_copy, "w3", 0)
-        regroup(nc.vector.tensor_copy, "w3", 1)
+        for i in range(2):
+            round_columns(nc.vector.tensor_copy, "w3", w3_raw[i], i * HALF, (i + 1) * HALF)
         quantize_first("w3", 2)
-        ring, side = bank[:RING], bank[RING:]
-        light(0, 0, ring[: T // BANK], nc.scalar.copy)
-        light(1, 0, ring[T // BANK :], nc.scalar.copy)
 
         w2_codes = keep.tile([P, N], U32, name="w2_codes", align_bytes=64)
         w2_plane = keep.tile([P, N], U8, name="w2_plane", align_bytes=64)
         w2_grouped = grouped["w3"][:, : PACK * N]
-        slot_codes[EARLY] = after_w3.tile([P, S - EARLY], U32, name="late_codes", align_bytes=64, offset=0)
-        nc.vector.tensor_copy(slot_codes[EARLY][:], x_codes[:].bitcast(U32).indirect(offsets[:, EARLY // 16 :]))
         nc.gpsimd.tensor_scalar(w2_grouped.rearrange("p (c j) -> p c j", j=PACK), w2_raw[:].rearrange("p j c -> p c j"), 1.0, 0.0, MULT, ADD)
 
         def first_product(name, g, acc):
@@ -135,14 +140,14 @@ def tile_moe_cas_glu_relu_kernel(tc, x_words, x_scales, w_words, w_scales, w1, w
                     out=acc[:, t * GROUP : (t + 1) * GROUP],
                     lhsT=codes[name][:, t * P : (t + 1) * P].bitcast(FP8X4),
                     lhsT_scale=plane[name][:, t * P : (t + 1) * P],
-                    rhs=words(g * GROUP, (g + 1) * GROUP),
+                    rhs=slot_codes[:, g * GROUP : (g + 1) * GROUP].bitcast(FP8X4),
                     rhs_scale=slot_plane[:, g * GROUP : (g + 1) * GROUP],
                     start=True,
                     stop=True,
                 )
             return acc[:].rearrange("p (t s) -> p s t", t=PACK)
 
-        gates = [keep.tile([P, GROUP * PACK], F32, name=f"gate{g}") for g in range(GROUPS)]
+        gates = [keep.tile([P, GROUP * PACK], F32, name=f"gate{g}") if g != 1 else after_w3.tile([P, GROUP * PACK], F32, name="gate1", offset=0) for g in range(GROUPS)]
         h = [keep.tile([P, CHUNK * PACK], BF16, name=f"h{c}", align_bytes=64) for c in range(CHUNKS)]
         h_codes = keep.tile([P, S], U32, name="h_codes", align_bytes=64)
         h_plane = keep.tile([P, S], U8, name="h_plane", align_bytes=64)
@@ -152,7 +157,11 @@ def tile_moe_cas_glu_relu_kernel(tc, x_words, x_scales, w_words, w_scales, w1, w
             return ap.rearrange("p (s t) -> p s t", t=PACK)
 
         def gate(g, acc):
-            nc.scalar.activation(out=by_slot(gates[g][:]), in_=first_product("w1", g, acc), func=RELU)
+            sums = first_product("w1", g, acc)
+            if g == 1:
+                nc.vector.tensor_scalar_max(by_slot(gates[g][:]), sums, 0.0)
+            else:
+                nc.scalar.activation(out=by_slot(gates[g][:]), in_=sums, func=RELU)
 
         def hidden(g, acc):
             lo = g % (CHUNK // GROUP) * GROUP * PACK
@@ -181,22 +190,29 @@ def tile_moe_cas_glu_relu_kernel(tc, x_words, x_scales, w_words, w_scales, w1, w
         def listed(b, lo, hi):
             return windows[b][:].indirect(offsets[:, lo // 16 : hi // 16])
 
+        gate_bank = [bank[i] for i in (7, 0, 1, 2, 3, 0, 4, 5)]
+        side = [bank[i] for i in (4, 5, 6, 7, 1, 2, 6, 7)]
+        for g in range(5):
+            gate(g, gate_bank[g])
         for g in range(GROUPS):
-            gate(g, ring[g % len(ring)])
-            hidden(g, side[g % len(side)])
+            hidden(g, side[g])
+            if g + 5 < GROUPS:
+                gate(g + 5, gate_bank[g + 5])
             if g == 1:
                 nc.vector.quantize_mx(out=w2_codes[:].bitcast(FP8X4), scales=w2_plane[:], in_=w2_grouped)
-            if g >= 2 and g % 2 == 0:
+                quantize_hidden(0)
+            if g in (4, 6):
                 quantize_hidden(g // 2 - 1)
-
-        light(1, 1, [ring[3]], nc.scalar.copy)
-        light(1, 2, [side[5 % len(side)], side[6 % len(side)]], nc.vector.tensor_copy)
+        light(1, SPLIT, SPLIT + BANK, side[5], nc.vector.tensor_copy)
+        light(1, SPLIT + BANK, T, side[6], nc.vector.tensor_copy)
         quantize_hidden(CHUNKS - 1)
 
-        for c, g in enumerate((6, 7, 4, 5)):
-            lo, hi = c * CHUNK, (c + 1) * CHUNK
-            results(c, ring[g % len(ring)])
+        def scatter_first(lo, hi):
             nc.scalar.activation(out=listed(0, lo, hi), in_=z[0][:, lo:hi], func=COPY)
+
+        for c, acc in enumerate(gate_bank[4:]):
+            results(c, acc)
+            scatter_first(c * CHUNK, (c + 1) * CHUNK)
         nc.scalar.dma_start(out=out[0:P, :], in_=windows[0][:])
 
         for lo in (0, S // 2):

@@ -27,8 +27,8 @@ GROUPS = S // GROUP
 CHUNK = 2 * GROUP
 CHUNKS = S // CHUNK
 W1_CUTS = (0, 192, 352, 512)
-HALF = H // 2
-SPLIT = 1280
+W3_CUTS = (0, 256, 384, 512)
+SPLIT = 1408
 
 
 def tile_moe_cas_glu_relu_kernel(tc, x_words, x_scales, w_words, w_scales, w1, w3, w2, offs, out):
@@ -57,7 +57,8 @@ def tile_moe_cas_glu_relu_kernel(tc, x_words, x_scales, w_words, w_scales, w1, w
 
         w1_cols = list(zip(W1_CUTS, W1_CUTS[1:]))
         w1_raw = [keep.tile([P, PACK, hi - lo], F32, name=f"w1_raw{lo}") for lo, hi in w1_cols]
-        w3_raw = [keep.tile([P, PACK, HALF], F32, name="w3_raw0"), after_w3.tile([P, PACK, HALF], F32, name="w3_raw1", offset=0)]
+        w3_cols = list(zip(W3_CUTS, W3_CUTS[1:]))
+        w3_raw = [keep.tile([P, PACK, hi - lo], F32, name=f"w3_raw{lo}") if hi < H else after_w3.tile([P, PACK, hi - lo], F32, name="w3_last", offset=0) for lo, hi in w3_cols]
         w2_raw = keep.tile([P, PACK, N], F32, name="w2_raw")
 
         grouped = {name: keep.tile([P, PACK * H], BF16, name=f"{name}_grouped", align_bytes=64) for name in ("w1", "w3")}
@@ -85,8 +86,8 @@ def tile_moe_cas_glu_relu_kernel(tc, x_words, x_scales, w_words, w_scales, w1, w
             load_scale_row(nc.sync, w_plane, w_scales, r)
         for i in (1, 2):
             load_columns(nc.sync, w1_raw[i], w1, *w1_cols[i])
-        for i in range(2):
-            load_columns(nc.sync, w3_raw[i], w3, i * HALF, (i + 1) * HALF)
+        for raw, cols in zip(w3_raw, w3_cols):
+            load_columns(nc.sync, raw, w3, *cols)
         nc.sync.dma_start(out=w2_raw[:], in_=w2.rearrange("(p j) c -> p j c", j=PACK))
 
         slot_plane = keep.tile([P, S], U8, name="slot_plane", align_bytes=64)
@@ -102,17 +103,21 @@ def tile_moe_cas_glu_relu_kernel(tc, x_words, x_scales, w_words, w_scales, w1, w
         windows = [keep.tile([P, T], F32, name=f"window{b}") for b in range(N // P)]
 
         def light(b, lo, hi, acc, copy):
-            cols = slice(lo, hi)
-            nc.tensor.matmul_mx(
-                out=acc[:, : hi - lo],
-                lhsT=w_codes[:, 2 * P * b : 2 * P * (b + 1)].bitcast(FP4X4),
-                lhsT_scale=w_plane[:, P * b : P * (b + 1)],
-                rhs=x_codes[:, cols].bitcast(FP8X4),
-                rhs_scale=x_plane[:, cols],
-                start=True,
-                stop=True,
-            )
-            copy(out=windows[b][:, cols], in_=acc[:, : hi - lo])
+            first = lo
+            for width in (512, 256, 128):
+                if (hi - lo) & width:
+                    cols = slice(first, first + width)
+                    nc.tensor.matmul_mx(
+                        out=acc[:, first - lo : first - lo + width],
+                        lhsT=w_codes[:, 2 * P * b : 2 * P * (b + 1)].bitcast(FP4X4),
+                        lhsT_scale=w_plane[:, P * b : P * (b + 1)],
+                        rhs=x_codes[:, cols].bitcast(FP8X4),
+                        rhs_scale=x_plane[:, cols],
+                        start=True,
+                        stop=True,
+                    )
+                    first += width
+            copy(out=windows[b][:, lo:hi], in_=acc[:, : hi - lo])
 
         def quantize_first(name, pieces):
             step = H // pieces
@@ -125,8 +130,8 @@ def tile_moe_cas_glu_relu_kernel(tc, x_words, x_scales, w_words, w_scales, w1, w
             light(*part, acc, nc.scalar.copy)
 
         quantize_first("w1", 1)
-        for i in range(2):
-            round_columns(nc.vector.tensor_copy, "w3", w3_raw[i], i * HALF, (i + 1) * HALF)
+        for raw, cols in zip(w3_raw, w3_cols):
+            round_columns(nc.vector.tensor_copy, "w3", raw, *cols)
         quantize_first("w3", 2)
 
         w2_codes = keep.tile([P, N], U32, name="w2_codes", align_bytes=64)

@@ -27,7 +27,7 @@ GROUPS = S // GROUP
 CHUNK = 2 * GROUP
 CHUNKS = S // CHUNK
 W1_CUTS = (0, 192, 352, 512)
-W3_CUTS = (0, 256, 384, 512)
+W3_CUTS = (0, 256, 512)
 SPLIT = 1408
 
 

@@ -13,10 +13,10 @@ U16 = mybir.dt.uint16
 U8 = mybir.dt.uint8
 FP8X4 = mybir.dt.float8_e4m3fn_x4
 FP4X4 = mybir.dt.float4_e2m1fn_x4
-RELU = mybir.ActivationFunctionType.Relu
 COPY = mybir.ActivationFunctionType.Copy
 MULT = mybir.AluOpType.mult
 ADD = mybir.AluOpType.add
+MAX = mybir.AluOpType.max
 
 P = 128
 PACK = 4
@@ -126,7 +126,7 @@ def tile_moe_cas_glu_relu_kernel(tc, x_words, x_scales, w_words, w_scales, w1, w
                 nc.vector.quantize_mx(out=codes[name][:, cols].bitcast(FP8X4), scales=plane[name][:, cols], in_=grouped[name][:, PACK * lo : PACK * (lo + step)])
 
         early = [(b, lo, min(lo + BANK, stop)) for b, stop in ((0, T), (1, SPLIT)) for lo in range(0, stop, BANK)]
-        for acc, part in zip(bank, early):
+        for acc, part in zip(bank, early[:5]):
             light(*part, acc, nc.scalar.copy)
 
         quantize_first("w1", 1)
@@ -163,15 +163,13 @@ def tile_moe_cas_glu_relu_kernel(tc, x_words, x_scales, w_words, w_scales, w1, w
 
         def gate(g, acc):
             sums = first_product("w1", g, acc)
-            if g == 1:
-                nc.vector.tensor_scalar_max(by_slot(gates[g][:]), sums, 0.0)
-            else:
-                nc.scalar.activation(out=by_slot(gates[g][:]), in_=sums, func=RELU)
+            copy = nc.vector.tensor_copy if g == 1 else nc.scalar.copy
+            copy(out=by_slot(gates[g][:]), in_=sums)
 
         def hidden(g, acc):
             lo = g % (CHUNK // GROUP) * GROUP * PACK
             part = h[g * GROUP // CHUNK][:, lo : lo + GROUP * PACK]
-            nc.vector.tensor_tensor(out=by_slot(part), in0=first_product("w3", g, acc), in1=by_slot(gates[g][:]), op=MULT)
+            nc.vector.scalar_tensor_tensor(out=by_slot(part), in0=by_slot(gates[g][:]), scalar=0.0, in1=first_product("w3", g, acc), op0=MAX, op1=MULT)
 
         def quantize_hidden(c):
             cols = slice(c * CHUNK, (c + 1) * CHUNK)
@@ -197,7 +195,10 @@ def tile_moe_cas_glu_relu_kernel(tc, x_words, x_scales, w_words, w_scales, w1, w
 
         gate_bank = [bank[i] for i in (7, 0, 1, 2, 3, 0, 4, 5)]
         side = [bank[i] for i in (4, 5, 6, 7, 1, 2, 6, 7)]
-        for g in range(5):
+        gate(0, gate_bank[0])
+        for acc, part in zip(bank[5:], early[5:]):
+            light(*part, acc, nc.scalar.copy)
+        for g in range(1, 5):
             gate(g, gate_bank[g])
         for g in range(GROUPS):
             hidden(g, side[g])

@@ -27,6 +27,7 @@ GROUPS = S // GROUP
 CHUNK = 2 * GROUP
 CHUNKS = S // CHUNK
 W1_CUTS = (0, 192, 352, 512)
+SCALAR_COLUMNS = 288
 W3_CUTS = (0, 256, 512)
 SPLIT = 1408
 
@@ -35,6 +36,7 @@ def tile_moe_cas_glu_relu_kernel(tc, x_words, x_scales, w_words, w_scales, w1, w
     nc = tc.nc
     with ExitStack() as ctx:
         keep = ctx.enter_context(tc.tile_pool(name="keep", bufs=1))
+        after_w1 = ctx.enter_context(tc.tile_pool(name="after_w1", bufs=1))
         after_w3 = ctx.enter_context(tc.tile_pool(name="after_w3", bufs=1))
         psum = ctx.enter_context(tc.psum_pool(name="psum", bufs=1))
 
@@ -56,7 +58,7 @@ def tile_moe_cas_glu_relu_kernel(tc, x_words, x_scales, w_words, w_scales, w1, w
             queue.dma_start(out=raw[:], in_=w[:, lo:hi].rearrange("(p j) c -> p j c", j=PACK))
 
         w1_cols = list(zip(W1_CUTS, W1_CUTS[1:]))
-        w1_raw = [keep.tile([P, PACK, hi - lo], F32, name=f"w1_raw{lo}") for lo, hi in w1_cols]
+        w1_raw = [keep.tile([P, PACK, hi - lo], F32, name=f"w1_raw{lo}") if lo != W1_CUTS[1] else after_w1.tile([P, PACK, hi - lo], F32, name="w1_second", offset=0) for lo, hi in w1_cols]
         w3_cols = list(zip(W3_CUTS, W3_CUTS[1:]))
         w3_raw = [keep.tile([P, PACK, hi - lo], F32, name=f"w3_raw{lo}") if hi < H else after_w3.tile([P, PACK, hi - lo], F32, name="w3_last", offset=0) for lo, hi in w3_cols]
         w2_raw = keep.tile([P, PACK, N], F32, name="w2_raw")
@@ -69,7 +71,7 @@ def tile_moe_cas_glu_relu_kernel(tc, x_words, x_scales, w_words, w_scales, w1, w
             whole = grouped[name][:].rearrange("p (t m j) -> p t m j", t=PACK, j=PACK)
             return (
                 whole[:, :, lo // PACK : hi // PACK, :].rearrange("p t m j -> p " + walk),
-                raw[:].rearrange("p j (m t) -> p " + walk, t=PACK),
+                raw.rearrange("p j (m t) -> p " + walk, t=PACK),
             )
 
         def round_columns(copy, name, raw, lo, hi):
@@ -95,12 +97,14 @@ def tile_moe_cas_glu_relu_kernel(tc, x_words, x_scales, w_words, w_scales, w1, w
         nc.vector.tensor_copy(slot_plane[:], x_plane[:].indirect(offsets[:]))
         nc.vector.tensor_copy(slot_codes[:], x_codes[:].bitcast(U32).indirect(offsets[:]))
 
-        round_columns(nc.scalar.copy, "w1", w1_raw[0], *w1_cols[0])
-        for i in (1, 2):
-            target, source = regrouped("w1", w1_raw[i], *w1_cols[i], "m t j")
+        share = SCALAR_COLUMNS - W1_CUTS[1]
+        round_columns(nc.scalar.copy, "w1", w1_raw[0][:], *w1_cols[0])
+        round_columns(nc.scalar.copy, "w1", w1_raw[1][:, :, :share], W1_CUTS[1], SCALAR_COLUMNS)
+        for raw, lo, hi in ((w1_raw[1][:, :, share:], SCALAR_COLUMNS, W1_CUTS[2]), (w1_raw[2][:], *w1_cols[2])):
+            target, source = regrouped("w1", raw, lo, hi, "m t j")
             nc.gpsimd.tensor_scalar(target, source, 1.0, 0.0, MULT, ADD)
 
-        windows = [keep.tile([P, T], F32, name=f"window{b}") for b in range(N // P)]
+        windows = [after_w1.tile([P, T], F32, name="window0", offset=0), keep.tile([P, T], F32, name="window1")]
 
         def light(b, lo, hi, acc, copy):
             first = lo
@@ -131,7 +135,7 @@ def tile_moe_cas_glu_relu_kernel(tc, x_words, x_scales, w_words, w_scales, w1, w
 
         quantize_first("w1", 1)
         for raw, cols in zip(w3_raw, w3_cols):
-            round_columns(nc.vector.tensor_copy, "w3", raw, *cols)
+            round_columns(nc.vector.tensor_copy, "w3", raw[:], *cols)
         quantize_first("w3", 2)
 
         w2_codes = keep.tile([P, N], U32, name="w2_codes", align_bytes=64)

@@ -29,7 +29,7 @@ CHUNKS = S // CHUNK
 W1_CUTS = (0, 192, 352, 512)
 SCALAR_COLUMNS = 288
 W3_CUTS = (0, 256, 512)
-SPLIT = 1408
+SPLIT = 1280
 
 
 def tile_moe_cas_glu_relu_kernel(tc, x_words, x_scales, w_words, w_scales, w1, w3, w2, offs, out):
@@ -197,8 +197,8 @@ def tile_moe_cas_glu_relu_kernel(tc, x_words, x_scales, w_words, w_scales, w1, w
         def listed(b, lo, hi):
             return windows[b][:].indirect(offsets[:, lo // 16 : hi // 16])
 
-        gate_bank = [bank[i] for i in (7, 0, 1, 2, 3, 0, 4, 5)]
-        side = [bank[i] for i in (4, 5, 6, 7, 1, 2, 6, 7)]
+        gate_bank = [bank[i] for i in (7, 0, 1, 2, 3, 0, 4, 7)]
+        side = [bank[i] for i in (4, 7, 5, 6, 1, 2, 5, 6)]
         gate(0, gate_bank[0])
         for acc, part in zip(bank[5:], early[5:]):
             light(*part, acc, nc.scalar.copy)

@@ -29,7 +29,7 @@ CHUNKS = S // CHUNK
 W1_CUTS = (0, 192, 352, 512)
 SCALAR_COLUMNS = 288
 W3_CUTS = (0, 256, 512)
-SPLIT = 1280
+SPLIT = 1152
 
 
 def tile_moe_cas_glu_relu_kernel(tc, x_words, x_scales, w_words, w_scales, w1, w3, w2, offs, out):
@@ -140,7 +140,7 @@ def tile_moe_cas_glu_relu_kernel(tc, x_words, x_scales, w_words, w_scales, w1, w
 
         w2_codes = keep.tile([P, N], U32, name="w2_codes", align_bytes=64)
         w2_plane = keep.tile([P, N], U8, name="w2_plane", align_bytes=64)
-        w2_grouped = grouped["w3"][:, : PACK * N]
+        w2_grouped = grouped["w3"][:, PACK * N :]
         nc.gpsimd.tensor_scalar(w2_grouped.rearrange("p (c j) -> p c j", j=PACK), w2_raw[:].rearrange("p j c -> p c j"), 1.0, 0.0, MULT, ADD)
 
         def first_product(name, g, acc):
@@ -227,4 +227,5 @@ def tile_moe_cas_glu_relu_kernel(tc, x_words, x_scales, w_words, w_scales, w1, w
 
         for lo in (0, S // 2):
             nc.vector.tensor_copy(listed(1, lo, lo + S // 2), z[1][:, lo : lo + S // 2])
-        nc.sync.dma_start(out=out[P : 2 * P, :], in_=windows[1][:])
+        nc.sync.dma_start(out=out[P : 2 * P, : T // 2], in_=windows[1][:, : T // 2])
+        nc.scalar.dma_start(out=out[P : 2 * P, T // 2 :], in_=windows[1][:, T // 2 :])

from contextlib import ExitStack

import concourse.mybir as mybir

K, T, S, H, N = 512, 2048, 1024, 512, 256
FLOPS = 2 * K * N * T + 2 * 2 * K * H * S + 2 * H * N * S

F32 = mybir.dt.float32
BF16 = mybir.dt.bfloat16
I32 = mybir.dt.int32
U32 = mybir.dt.uint32
U16 = mybir.dt.uint16
U8 = mybir.dt.uint8
FP8X4 = mybir.dt.float8_e4m3fn_x4
FP4X4 = mybir.dt.float4_e2m1fn_x4
COPY = mybir.ActivationFunctionType.Copy
MULT = mybir.AluOpType.mult
ADD = mybir.AluOpType.add
MAX = mybir.AluOpType.max

P = 128
PACK = 4
BANK = 512
BANKS = 8
GROUP = BANK // PACK
GROUPS = S // GROUP
CHUNK = 2 * GROUP
CHUNKS = S // CHUNK
W1_CUTS = (0, 192, 352, 512)
SCALAR_COLUMNS = 288
W3_CUTS = (0, 256, 512)
SPLIT = 1152


def tile_moe_cas_glu_relu_kernel(tc, x_words, x_scales, w_words, w_scales, w1, w3, w2, offs, out):
    nc = tc.nc
    with ExitStack() as ctx:
        keep = ctx.enter_context(tc.tile_pool(name="keep", bufs=1))
        after_w1 = ctx.enter_context(tc.tile_pool(name="after_w1", bufs=1))
        after_w3 = ctx.enter_context(tc.tile_pool(name="after_w3", bufs=1))
        psum = ctx.enter_context(tc.psum_pool(name="psum", bufs=1))

        bank = [psum.tile([P, BANK], F32, name=f"bank{i}") for i in range(BANKS)]

        offsets = keep.tile([P, S // 16], U16, name="offsets")
        x_plane = keep.tile([P, T], U8, name="x_plane", align_bytes=64)
        w_plane = keep.tile([P, N], U8, name="w_plane", align_bytes=64)
        x_codes = keep.tile([P, T], I32, name="x_codes", align_bytes=64)
        w_codes = keep.tile([P, 2 * N], U8, name="w_codes", align_bytes=64)
        nc.vector.memset(x_plane[:].bitcast(I32), 0)
        nc.vector.memset(w_plane[:].bitcast(I32), 0)

        def load_scale_row(queue, target, scales, r):
            rows = scales[0].rearrange("(q r) c -> r q c", r=4)
            queue.dma_start(out=target[r:P:32, :].bitcast(I32), in_=rows[r].bitcast(I32))

        def load_columns(queue, raw, w, lo, hi):
            queue.dma_start(out=raw[:], in_=w[:, lo:hi].rearrange("(p j) c -> p j c", j=PACK))

        w1_cols = list(zip(W1_CUTS, W1_CUTS[1:]))
        w1_raw = [keep.tile([P, PACK, hi - lo], F32, name=f"w1_raw{lo}") if lo != W1_CUTS[1] else after_w1.tile([P, PACK, hi - lo], F32, name="w1_second", offset=0) for lo, hi in w1_cols]
        w3_cols = list(zip(W3_CUTS, W3_CUTS[1:]))
        w3_raw = [keep.tile([P, PACK, hi - lo], F32, name=f"w3_raw{lo}") if hi < H else after_w3.tile([P, PACK, hi - lo], F32, name="w3_last", offset=0) for lo, hi in w3_cols]
        w2_raw = keep.tile([P, PACK, N], F32, name="w2_raw")

        grouped = {name: keep.tile([P, PACK * H], BF16, name=f"{name}_grouped", align_bytes=64) for name in ("w1", "w3")}
        codes = {name: keep.tile([P, H], U32, name=f"{name}_codes", align_bytes=64) for name in ("w1", "w3")}
        plane = {name: keep.tile([P, H], U8, name=f"{name}_plane", align_bytes=64) for name in ("w1", "w3")}

        def regrouped(name, raw, lo, hi, walk):
            whole = grouped[name][:].rearrange("p (t m j) -> p t m j", t=PACK, j=PACK)
            return (
                whole[:, :, lo // PACK : hi // PACK, :].rearrange("p t m j -> p " + walk),
                raw.rearrange("p j (m t) -> p " + walk, t=PACK),
            )

        def round_columns(copy, name, raw, lo, hi):
            target, source = regrouped(name, raw, lo, hi, "m j t")
            copy(out=target, in_=source)

        load_columns(nc.sync, w1_raw[0], w1, *w1_cols[0])
        nc.sync.dma_start(offsets[:], offs)
        nc.sync.dma_start(out=w_codes[:].bitcast(I32), in_=w_words[0].bitcast(I32))
        for r in range(4):
            load_scale_row(nc.sync, x_plane, x_scales, r)
        nc.sync.dma_start(out=x_codes[:], in_=x_words[0].rearrange("p t d -> p (t d)").bitcast(I32))
        for r in range(4):
            load_scale_row(nc.sync, w_plane, w_scales, r)
        for i in (1, 2):
            load_columns(nc.sync, w1_raw[i], w1, *w1_cols[i])
        for raw, cols in zip(w3_raw, w3_cols):
            load_columns(nc.sync, raw, w3, *cols)
        nc.sync.dma_start(out=w2_raw[:], in_=w2.rearrange("(p j) c -> p j c", j=PACK))

        slot_plane = keep.tile([P, S], U8, name="slot_plane", align_bytes=64)
        slot_codes = keep.tile([P, S], U32, name="slot_codes", align_bytes=64)
        nc.vector.tensor_copy(slot_plane[:], x_plane[:].indirect(offsets[:]))
        nc.vector.tensor_copy(slot_codes[:], x_codes[:].bitcast(U32).indirect(offsets[:]))

        share = SCALAR_COLUMNS - W1_CUTS[1]
        round_columns(nc.scalar.copy, "w1", w1_raw[0][:], *w1_cols[0])
        round_columns(nc.scalar.copy, "w1", w1_raw[1][:, :, :share], W1_CUTS[1], SCALAR_COLUMNS)
        for raw, lo, hi in ((w1_raw[1][:, :, share:], SCALAR_COLUMNS, W1_CUTS[2]), (w1_raw[2][:], *w1_cols[2])):
            target, source = regrouped("w1", raw, lo, hi, "m t j")
            nc.gpsimd.tensor_scalar(target, source, 1.0, 0.0, MULT, ADD)

        windows = [after_w1.tile([P, T], F32, name="window0", offset=0), keep.tile([P, T], F32, name="window1")]

        def light(b, lo, hi, acc, copy):
            first = lo
            for width in (512, 256, 128):
                if (hi - lo) & width:
                    cols = slice(first, first + width)
                    nc.tensor.matmul_mx(
                        out=acc[:, first - lo : first - lo + width],
                        lhsT=w_codes[:, 2 * P * b : 2 * P * (b + 1)].bitcast(FP4X4),
                        lhsT_scale=w_plane[:, P * b : P * (b + 1)],
                        rhs=x_codes[:, cols].bitcast(FP8X4),
                        rhs_scale=x_plane[:, cols],
                        start=True,
                        stop=True,
                    )
                    first += width
            copy(out=windows[b][:, lo:hi], in_=acc[:, : hi - lo])

        def quantize_first(name, pieces):
            step = H // pieces
            for lo in reversed(range(0, H, step)):
                cols = slice(lo, lo + step)
                nc.vector.quantize_mx(out=codes[name][:, cols].bitcast(FP8X4), scales=plane[name][:, cols], in_=grouped[name][:, PACK * lo : PACK * (lo + step)])

        early = [(b, lo, min(lo + BANK, stop)) for b, stop in ((0, T), (1, SPLIT)) for lo in range(0, stop, BANK)]
        for acc, part in zip(bank, early[:5]):
            light(*part, acc, nc.scalar.copy)

        quantize_first("w1", 1)
        for raw, cols in zip(w3_raw, w3_cols):
            round_columns(nc.vector.tensor_copy, "w3", raw[:], *cols)
        quantize_first("w3", 2)

        w2_codes = keep.tile([P, N], U32, name="w2_codes", align_bytes=64)
        w2_plane = keep.tile([P, N], U8, name="w2_plane", align_bytes=64)
        w2_grouped = grouped["w3"][:, PACK * N :]
        nc.gpsimd.tensor_scalar(w2_grouped.rearrange("p (c j) -> p c j", j=PACK), w2_raw[:].rearrange("p j c -> p c j"), 1.0, 0.0, MULT, ADD)

        def first_product(name, g, acc):
            for t in reversed(range(PACK)):
                nc.tensor.matmul_mx(
                    out=acc[:, t * GROUP : (t + 1) * GROUP],
                    lhsT=codes[name][:, t * P : (t + 1) * P].bitcast(FP8X4),
                    lhsT_scale=plane[name][:, t * P : (t + 1) * P],
                    rhs=slot_codes[:, g * GROUP : (g + 1) * GROUP].bitcast(FP8X4),
                    rhs_scale=slot_plane[:, g * GROUP : (g + 1) * GROUP],
                    start=True,
                    stop=True,
                )
            return acc[:].rearrange("p (t s) -> p s t", t=PACK)

        gates = [keep.tile([P, GROUP * PACK], F32, name=f"gate{g}") if g != 1 else after_w3.tile([P, GROUP * PACK], F32, name="gate1", offset=0) for g in range(GROUPS)]
        h = [keep.tile([P, CHUNK * PACK], BF16, name=f"h{c}", align_bytes=64) for c in range(CHUNKS)]
        h_codes = keep.tile([P, S], U32, name="h_codes", align_bytes=64)
        h_plane = keep.tile([P, S], U8, name="h_plane", align_bytes=64)
        z = [keep.tile([P, S], F32, name=f"z{b}") for b in range(N // P)]

        def by_slot(ap):
            return ap.rearrange("p (s t) -> p s t", t=PACK)

        def gate(g, acc):
            sums = first_product("w1", g, acc)
            copy = nc.vector.tensor_copy if g == 1 else nc.scalar.copy
            copy(out=by_slot(gates[g][:]), in_=sums)

        def hidden(g, acc):
            lo = g % (CHUNK // GROUP) * GROUP * PACK
            part = h[g * GROUP // CHUNK][:, lo : lo + GROUP * PACK]
            nc.vector.scalar_tensor_tensor(out=by_slot(part), in0=by_slot(gates[g][:]), scalar=0.0, in1=first_product("w3", g, acc), op0=MAX, op1=MULT)

        def quantize_hidden(c):
            cols = slice(c * CHUNK, (c + 1) * CHUNK)
            nc.vector.quantize_mx(out=h_codes[:, cols].bitcast(FP8X4), scales=h_plane[:, cols], in_=h[c][:])

        def results(c, acc):
            lo, hi = c * CHUNK, (c + 1) * CHUNK
            for b in range(N // P):
                nc.tensor.matmul_mx(
                    out=acc[:, b * CHUNK : (b + 1) * CHUNK],
                    lhsT=w2_codes[:, b * P : (b + 1) * P].bitcast(FP8X4),
                    lhsT_scale=w2_plane[:, b * P : (b + 1) * P],
                    rhs=h_codes[:, lo:hi].bitcast(FP8X4),
                    rhs_scale=h_plane[:, lo:hi],
                    start=True,
                    stop=True,
                )
            for b in range(N // P):
                nc.scalar.copy(out=z[b][:, lo:hi], in_=acc[:, b * CHUNK : (b + 1) * CHUNK])

        def listed(b, lo, hi):
            return windows[b][:].indirect(offsets[:, lo // 16 : hi // 16])

        gate_bank = [bank[i] for i in (7, 0, 1, 2, 3, 0, 4, 7)]
        side = [bank[i] for i in (4, 7, 5, 6, 1, 2, 5, 6)]
        gate(0, gate_bank[0])
        for acc, part in zip(bank[5:], early[5:]):
            light(*part, acc, nc.scalar.copy)
        for g in range(1, 5):
            gate(g, gate_bank[g])
        for g in range(GROUPS):
            hidden(g, side[g])
            if g + 5 < GROUPS:
                gate(g + 5, gate_bank[g + 5])
            if g == 1:
                nc.vector.quantize_mx(out=w2_codes[:].bitcast(FP8X4), scales=w2_plane[:], in_=w2_grouped)
                quantize_hidden(0)
            if g in (4, 6):
                quantize_hidden(g // 2 - 1)
        light(1, SPLIT, SPLIT + BANK, side[5], nc.vector.tensor_copy)
        light(1, SPLIT + BANK, T, side[6], nc.vector.tensor_copy)
        quantize_hidden(CHUNKS - 1)

        def scatter_first(lo, hi):
            nc.scalar.activation(out=listed(0, lo, hi), in_=z[0][:, lo:hi], func=COPY)

        for c, acc in enumerate(gate_bank[4:]):
            results(c, acc)
            scatter_first(c * CHUNK, (c + 1) * CHUNK)
        nc.scalar.dma_start(out=out[0:P, :], in_=windows[0][:])

        for lo in (0, S // 2):
            nc.vector.tensor_copy(listed(1, lo, lo + S // 2), z[1][:, lo : lo + S // 2])
        nc.sync.dma_start(out=out[P : 2 * P, : T // 2], in_=windows[1][:, : T // 2])
        nc.scalar.dma_start(out=out[P : 2 * P, T // 2 :], in_=windows[1][:, T // 2 :])
